import numpy as np
import ml_dtypes


def mxq(x, axis, fmt="e4m3"):
    dtype, down = {"e4m3": (ml_dtypes.float8_e4m3fn, 7), "e5m2": (ml_dtypes.float8_e5m2, 14)}[fmt]
    v = np.moveaxis(np.asarray(x, np.float32).astype(ml_dtypes.bfloat16).astype(np.float64), axis, -1)
    blocks = v.reshape(v.shape[:-1] + (-1, 32))
    amax = np.abs(blocks).max(-1, keepdims=True)
    byte = np.maximum(np.where(amax > 0, np.frexp(amax)[1] - 1 + 127, 0) - down, 1)
    scale = np.exp2(byte - 127.0)
    codes = (blocks / scale).astype(np.float32).astype(dtype).astype(np.float64)
    return np.moveaxis((codes * scale).reshape(v.shape), -1, axis)


WIDE = False


def mx_kscale(k):
    if not WIDE:
        return np.ones(k)
    levels = np.array([10, -10, 5, -5, 0])
    if k % 512:
        return np.exp2(np.random.permutation(np.resize(levels, k // 32))).repeat(32)
    a = np.empty((k // 512, 16))
    for p in range(k // 512):
        a[p, :8] = np.random.permutation(np.resize(levels, 8))
        for g in range(8):
            far = levels[np.abs(levels - a[p, g]) >= 10]
            a[p, g + 8] = far[np.random.randint(len(far))]
    return np.exp2(a.ravel()).repeat(32)


BF16 = ml_dtypes.bfloat16


def bf(x):
    return np.asarray(x, np.float32).astype(BF16)


def f64(x):
    return np.asarray(x).astype(np.float64)


N, D, F = 1024, 2048, 1024
H = F // 2


def max_min(h):
    hl = h[:, :H]
    hr = h[:, H:]
    return np.concatenate([np.maximum(hl, hr), np.minimum(hl, hr)], axis=1)


def draw0():
    a, u = mx_kscale(D), mx_kscale(F)
    return {
        "x": bf(np.random.standard_normal((N, D)) * a[None, :]),
        "w": bf(np.random.standard_normal((D, F)) / np.sqrt(D) / a[:, None]),
        "d": bf((1.0 + 0.2 * np.random.standard_normal(D)) * a * a),
        "s": bf((1.0 + 0.1 * np.random.standard_normal(F)) * u),
        "t": bf((1.0 + 0.1 * np.random.standard_normal(F)) / u),
        "b": bf(0.4 * np.random.standard_normal(F)),
    }


def core(x, w, d, s, t, b):
    x, w, d, s, t, b = f64(x), f64(w), f64(d), f64(s), f64(t), f64(b)
    wq = mxq(w, 0, "e4m3")
    p = mxq(x, 1, "e4m3") @ wq
    wd = d[:, None] * w
    g = mxq(wd, 0, "e4m3").T @ wq
    ps = p * s[None, :]
    gt = g * t[:, None]
    r = mxq(ps, 1, "e4m3") @ mxq(gt, 0, "e4m3")
    h = 1.5 * p - 0.5 * r + b[None, :]
    return max_min(h)


def e4m3fn_bytes(y):
    return np.clip(np.asarray(y, np.float64), -448.0, 448.0).astype(np.float32).astype(ml_dtypes.float8_e4m3fn).view(np.uint8)


def e4m3fn_values(b):
    return np.asarray(b, np.uint8).view(ml_dtypes.float8_e4m3fn).astype(np.float64)


def setup_inputs():
    d = draw0()
    x0 = np.asarray(d['x']).astype(np.float64)
    s = (np.max(np.abs(x0), axis=(0,), keepdims=True) / 448.0).astype(np.float32)
    out = {}
    for k, v in d.items():
        if k == 'x':
            out['x_bytes'] = e4m3fn_bytes(x0 / s.astype(np.float64))
            out['x_scale'] = s
        else:
            out[k] = v
    return out


def reference(x_bytes, x_scale, w, d, s, t, b):
    return core(e4m3fn_values(x_bytes) * x_scale.astype(np.float64), w, d, s, t, b)

@@ -1,0 +1,491 @@
+from contextlib import ExitStack
+
+import concourse.mybir as mybir
+from concourse.masks import make_identity
+
+F32 = mybir.dt.float32
+BF16 = mybir.dt.bfloat16
+U32 = mybir.dt.uint32
+U8 = mybir.dt.uint8
+FP8 = mybir.dt.float8_e4m3fn
+FP8X4 = mybir.dt.float8_e4m3fn_x4
+ALU = mybir.AluOpType
+ACT = mybir.ActivationFunctionType
+
+P = 128
+N, D, F = 1024, 2048, 1024
+KP = D // 512
+CH = F // 512
+FLOPS = 2 * N * D * F + 2 * D * F * F + 2 * N * F * F
+
+
+def tile_bjorckmaxmindense_kernel(tc, x_bytes, x_scale, w, d, s, t, b, out):
+    nc = tc.nc
+    with ExitStack() as ctx:
+        const = ctx.enter_context(tc.tile_pool(name="const", bufs=1))
+        pool = ctx.enter_context(tc.tile_pool(name="pool", bufs=2))
+        psum = ctx.enter_context(tc.psum_pool(name="psum", bufs=1))
+
+        T = {}
+
+        def big(key, shape, dt, tag, bufs):
+            if key not in T:
+                tl = pool.tile(shape, dt, name=tag, tag=tag, bufs=bufs, align_bytes=64)
+                T[key] = tl
+            return T[key]
+
+        def bank(key, shape, tag, bufs, dt=F32):
+            if key not in T:
+                tl = psum.tile(shape, dt, name=tag, tag=tag, bufs=bufs)
+                T[key] = tl
+            return T[key]
+
+        sc = const.tile([P, D], F32, align_bytes=64)
+        d_sb = const.tile([P, KP, 4], BF16)
+        nc.gpsimd.dma_start(out=d_sb[:], in_=d.rearrange("(g p j) -> p g j", p=P, j=4))
+        vec32 = []
+        for i, v in enumerate((t, s, b)):
+            v16 = const.tile([P, CH, 4], BF16, name="v16_%d" % i)
+            nc.gpsimd.dma_start(out=v16[:], in_=v.rearrange("(c m t) -> m c t", m=P, t=4))
+            v32 = const.tile([P, CH, 4], F32, name="v32_%d" % i)
+            nc.gpsimd.tensor_copy(out=v32[:], in_=v16[:])
+            vec32.append(v32)
+        ident = const.tile([P, P], F32)
+        make_identity(nc, ident[:])
+        wq = const.tile([P, KP, F], U32, align_bytes=64)
+        wqs = const.tile([P, KP, F], U8, align_bytes=64)
+        wdqs = const.tile([P, KP, F], U8, align_bytes=64)
+        xq = const.tile([P, 2, KP, 512], U32, align_bytes=64)
+        xqs = const.tile([P, 2, KP, 512], U8, align_bytes=64)
+        gtq = const.tile([P, CH, F], U32, align_bytes=64)
+        gtqs = const.tile([P, CH, F], U8, align_bytes=64)
+        psq = const.tile([P, CH, N], U32, align_bytes=64)
+        psqs = const.tile([P, CH, N], U8, align_bytes=64)
+
+        def LW(kp):
+            w_raw = big(("wr", kp), [P, 4, F], BF16, "w8", 4)
+            src = w[512 * kp : 512 * (kp + 1), :].rearrange("(p j) f -> p j f", j=4)
+            for c in range(CH):
+                nc.sync.dma_start(out=w_raw[:, :, 512 * c : 512 * (c + 1)], in_=src[:, :, 512 * c : 512 * (c + 1)])
+
+        def LX(i):
+            xb = big(("xb", i), [P, D], U8, "xb", 4)
+            nc.sync.dma_start(out=xb[:], in_=x_bytes[P * i : P * (i + 1), :])
+
+        def LSC():
+            nc.sync.dma_start(out=sc[:], in_=x_scale.rearrange("o k -> (o k)").partition_broadcast(P))
+
+        def wg_of(kp):
+            return big(("wg", kp), [P, CH, 4, P, 4], BF16, "g8", 5)
+
+        def WI(kp, c, t0, n, e):
+            srcv = T["wr", kp][:].rearrange("p j (c m t) -> p c t m j", c=CH, t=4)
+            o, i = wg_of(kp)[:, c, t0 : t0 + n], srcv[:, c, t0 : t0 + n]
+            if e == "S":
+                nc.scalar.copy(out=o, in_=i)
+            else:
+                nc.vector.tensor_copy(out=o, in_=i)
+
+        def WQ(kp):
+            nc.vector.quantize_mx(
+                out=wq[:, kp, :].bitcast(FP8X4), scales=wqs[:, kp, :], in_=wg_of(kp)[:].rearrange("p c t m j -> p (c t m j)")
+            )
+
+        def WD(kp):
+            wdg = big(("wdg", kp), [P, F, 4], BF16, "g8", 5)
+            nc.vector.tensor_tensor(
+                out=wdg[:],
+                in0=wg_of(kp)[:].rearrange("p c t m j -> p (c t m) j"),
+                in1=d_sb[:, kp : kp + 1, :].to_broadcast([P, F, 4]),
+                op=ALU.mult,
+            )
+
+        def WDQ(kp):
+            dq = big(("wdq", kp), [P, F], U32, "wdq", 4)
+            nc.vector.quantize_mx(
+                out=dq[:].bitcast(FP8X4), scales=wdqs[:, kp, :], in_=T["wdg", kp][:].rearrange("p f j -> p (f j)")
+            )
+
+        def XP(i):
+            xs = big(("xs", i), [P, D], BF16, "xs", 2)
+            nc.vector.tensor_tensor(out=xs[:], in0=T["xb", i][:].bitcast(FP8), in1=sc[:], op=ALU.mult)
+
+        def XT(i):
+            words = T["xs", i][:].bitcast(F32)
+            for g2 in range(2):
+                xt = bank(("xt", i, g2), [P, 2, 2, P], "tr", 3)
+                for gi in range(2):
+                    kp = 2 * g2 + gi
+                    for u in range(2):
+                        nc.tensor.transpose(xt[:, gi, u, :], words[:, 256 * kp + u : 256 * (kp + 1) : 2], ident[:])
+
+        def XC(i):
+            xg = big(("xg", i // 4), [P, KP, 512, 4], BF16, "xg", 2)
+            r = P * (i % 4)
+            for g2 in range(2):
+                nc.scalar.copy(
+                    out=xg[:].bitcast(F32)[:, 2 * g2 : 2 * g2 + 2, r : r + P, :],
+                    in_=T["xt", i, g2][:].rearrange("p g u r -> p g r u"),
+                )
+
+        def XQ(h):
+            xg = T["xg", h]
+            for k2 in range(2):
+                ks = slice(2 * k2, 2 * k2 + 2)
+                nc.vector.quantize_mx(
+                    out=xq[:, h, ks, :].rearrange("p k n -> p (k n)").bitcast(FP8X4),
+                    scales=xqs[:, h, ks, :].rearrange("p k n -> p (k n)"),
+                    in_=xg[:, ks].rearrange("p k n t -> p (k n t)"),
+                )
+
+        def PM(h, ct, kps=range(KP)):
+            acc = bank(("pa", h, ct), [P, 512], "acc", 5)
+            sl = slice(P * ct, P * (ct + 1))
+            for kp in kps:
+                nc.tensor.matmul_mx(
+                    out=acc[:],
+                    lhsT=wq[:, kp, sl].bitcast(FP8X4),
+                    lhsT_scale=wqs[:, kp, sl],
+                    rhs=xq[:, h, kp, :].bitcast(FP8X4),
+                    rhs_scale=xqs[:, h, kp, :],
+                    start=(kp == 0),
+                    stop=(kp == KP - 1),
+                )
+
+        def PC(h, ct):
+            c, tt = ct // 4, ct % 4
+            acc = T["pa", h, ct]
+            pl = big(("ppl", h, c), [P, 4, 512], BF16, "b4", 6)
+            pb = big(("p15", h, c), [P, 4, 512], F32, "w8", 4)
+            nc.scalar.activation(out=pl[:, tt, :], in_=acc[:], func=ACT.Copy, scale=vec32[1][:, c, tt : tt + 1])
+            nc.scalar.activation(
+                out=pb[:, tt, :], in_=acc[:], func=ACT.Identity, scale=1.5, bias=vec32[2][:, c, tt : tt + 1]
+            )
+
+        def ILV(src, key, e):
+            gg = big(key, [P, 512, 4], BF16, "b4", 6)
+            if e == "S":
+                nc.scalar.copy(out=gg[:], in_=src[:].rearrange("p t n -> p n t"))
+            else:
+                nc.vector.tensor_copy(out=gg[:], in_=src[:].rearrange("p t n -> p n t"))
+
+        def PI(h, c, e="V"):
+            ILV(T["ppl", h, c], ("pg", h, c), e)
+
+        def PQ(h, c):
+            tok = slice(512 * h, 512 * (h + 1))
+            nc.vector.quantize_mx(
+                out=psq[:, c, tok].bitcast(FP8X4), scales=psqs[:, c, tok], in_=T["pg", h, c][:].rearrange("p n t -> p (n t)")
+            )
+
+        def G(c, hh, tt, kps=range(KP)):
+            acc = bank(("ga", c, hh, tt), [P, 512], "acc", 5)
+            sl = slice(512 * c + P * tt, 512 * c + P * (tt + 1))
+            cols = slice(512 * hh, 512 * (hh + 1))
+            for kp in kps:
+                nc.tensor.matmul_mx(
+                    out=acc[:],
+                    lhsT=T["wdq", kp][:, sl].bitcast(FP8X4),
+                    lhsT_scale=wdqs[:, kp, sl],
+                    rhs=wq[:, kp, cols].bitcast(FP8X4),
+                    rhs_scale=wqs[:, kp, cols],
+                    start=(kp == 0),
+                    stop=(kp == KP - 1),
+                )
+
+        def GC(c, hh, tt):
+            pl = big(("gpl", c, hh), [P, 4, 512], BF16, "b4", 6)
+            nc.scalar.activation(
+                out=pl[:, tt, :], in_=T["ga", c, hh, tt][:], func=ACT.Copy, scale=vec32[0][:, c, tt : tt + 1]
+            )
+
+        def GI(c, hh, e="V"):
+            ILV(T["gpl", c, hh], ("gg", c, hh), e)
+
+        def GQ(c, hh):
+            cols = slice(512 * hh, 512 * (hh + 1))
+            nc.vector.quantize_mx(
+                out=gtq[:, c, cols].bitcast(FP8X4), scales=gtqs[:, c, cols], in_=T["gg", c, hh][:].rearrange("p n t -> p (n t)")
+            )
+
+        def R(q, c, tp):
+            acc = bank(("ra", q, c, tp), [P, 2, 256], "acc", 5)
+            tok = slice(256 * q, 256 * (q + 1))
+            for ti in range(2):
+                tt = 2 * tp + ti
+                sl = slice(512 * c + P * tt, 512 * c + P * (tt + 1))
+                for kc in range(CH):
+                    nc.tensor.matmul_mx(
+                        out=acc[:, ti, :],
+                        lhsT=gtq[:, kc, sl].bitcast(FP8X4),
+                        lhsT_scale=gtqs[:, kc, sl],
+                        rhs=psq[:, kc, tok].bitcast(FP8X4),
+                        rhs_scale=psqs[:, kc, tok],
+                        start=(kc == 0),
+                        stop=(kc == CH - 1),
+                    )
+
+        def ST(q, c, tp, e="V"):
+            ht = big(("ht", q, c), [P, 4, 256], F32, "wdq", 4)
+            off = 256 * (q % 2)
+            acc = T["ra", q, c, tp]
+            o = ht[:, 2 * tp : 2 * tp + 2, :]
+            p15 = T["p15", q // 2, c][:, 2 * tp : 2 * tp + 2, off : off + 256]
+            if e == "V":
+                nc.vector.scalar_tensor_tensor(out=o, in0=acc[:], scalar=-0.5, in1=p15, op0=ALU.mult, op1=ALU.add)
+            else:
+                rs = big(("rs", q, c, tp), [P, 2, 256], F32, "hr", 3)
+                nc.scalar.activation(out=rs[:], in_=acc[:], func=ACT.Copy, scale=-0.5)
+                nc.gpsimd.tensor_tensor(out=o, in0=rs[:], in1=p15, op=ALU.add)
+
+        def OT(q, i, c):
+            bk = bank(("ot", q, i, c), [P, 4, P], "tr", 3)
+            for tt in range(4):
+                nc.tensor.transpose(bk[:, tt, :], T["ht", q, c][:, tt, P * i : P * (i + 1)], ident[:])
+
+        def HR(q, i):
+            hr = big(("hr", q, i), [P, P, 4], F32, "hr", 2)
+            nc.scalar.copy(out=hr[:], in_=T["ot", q, i, 1][:].rearrange("p t m -> p m t"))
+
+        def MM(q, i):
+            blk = 2 * q + i
+            o = big(("o", q, i), [P, 2, P, 4], F32, "b4", 6)
+            hl = T["ot", q, i, 0][:].rearrange("p t m -> p m t")
+            hr = T["hr", q, i]
+            nc.vector.tensor_tensor(out=o[:, 0], in0=hl, in1=hr[:], op=ALU.max)
+            nc.vector.tensor_tensor(out=o[:, 1], in0=hl, in1=hr[:], op=ALU.min)
+            nc.sync.dma_start(out=out[P * blk : P * (blk + 1), :], in_=o[:].rearrange("p c m t -> p (c m t)"))
+
+        LW(0)
+        LSC()
+        LX(0)
+        LX(1)
+        LW(1)
+        LX(2)
+        LX(3)
+        LW(2)
+        LW(3)
+        LX(4)
+        LX(5)
+        LX(6)
+        LX(7)
+        WI(0, 0, 0, 4, "S")
+        WI(0, 1, 0, 4, "V")
+        WQ(0)
+        XP(0)
+        XT(0)
+        XP(1)
+        XT(1)
+        WI(1, 0, 0, 4, "S")
+        WI(1, 1, 0, 1, "V")
+        XC(0)
+        WI(1, 1, 1, 3, "S")
+        XC(1)
+        XP(2)
+        XT(2)
+        WQ(1)
+        WI(2, 0, 0, 4, "S")
+        WI(2, 1, 0, 1, "V")
+        WI(2, 1, 1, 3, "S")
+        XC(2)
+        XP(3)
+        XT(3)
+        WQ(2)
+        WI(3, 1, 0, 1, "V")
+        XC(3)
+        WI(3, 0, 0, 4, "S")
+        WI(3, 1, 1, 3, "S")
+        XQ(0)
+        PM(0, 0, [0])
+        PM(0, 1, [0])
+        PM(0, 2, [0])
+        PM(0, 3, [0])
+        PM(0, 4, [0])
+        PM(0, 0, [1])
+        PM(0, 1, [1])
+        PM(0, 2, [1])
+        PM(0, 3, [1])
+        PM(0, 4, [1])
+        PM(0, 0, [2])
+        PM(0, 1, [2])
+        PM(0, 2, [2])
+        PM(0, 3, [2])
+        PM(0, 4, [2])
+        WD(0)
+        WQ(3)
+        WDQ(0)
+        PM(0, 0, [3])
+        PM(0, 1, [3])
+        PM(0, 2, [3])
+        PM(0, 3, [3])
+        PM(0, 4, [3])
+        PC(0, 0)
+        PC(0, 1)
+        PC(0, 2)
+        PC(0, 3)
+        PC(0, 4)
+        PM(0, 5)
+        PC(0, 5)
+        PM(0, 6)
+        PC(0, 6)
+        PM(0, 7)
+        PC(0, 7)
+        WD(1)
+        WDQ(1)
+        WD(2)
+        WDQ(2)
+        PI(0, 0)
+        WD(3)
+        PQ(0, 0)
+        WDQ(3)
+        G(0, 0, 0, [0])
+        G(0, 0, 1, [0])
+        G(0, 0, 2, [0])
+        G(0, 0, 3, [0])
+        G(0, 0, 0, [1])
+        G(0, 0, 1, [1])
+        G(0, 0, 2, [1])
+        G(0, 0, 3, [1])
+        G(0, 0, 0, [2])
+        G(0, 0, 1, [2])
+        G(0, 0, 2, [2])
+        G(0, 0, 3, [2])
+        G(0, 0, 0, [3])
+        G(0, 0, 1, [3])
+        G(0, 0, 2, [3])
+        G(0, 0, 3, [3])
+        XP(4)
+        XT(4)
+        PI(0, 1)
+        XP(5)
+        PQ(0, 1)
+        XT(5)
+        GC(0, 0, 0)
+        GC(0, 0, 1)
+        GC(0, 0, 2)
+        GC(0, 0, 3)
+        G(1, 0, 0)
+        G(1, 0, 1)
+        G(1, 0, 2)
+        G(1, 0, 3)
+        XC(4)
+        XC(5)
+        GC(1, 0, 0)
+        GC(1, 0, 1)
+        GC(1, 0, 2)
+        GC(1, 0, 3)
+        GI(0, 0)
+        XP(6)
+        XT(6)
+        GQ(0, 0)
+        G(0, 1, 0)
+        G(0, 1, 1)
+        G(0, 1, 2)
+        G(0, 1, 3)
+        XC(6)
+        GI(1, 0)
+        GC(0, 1, 0)
+        GC(0, 1, 1)
+        GC(0, 1, 2)
+        GC(0, 1, 3)
+        XP(7)
+        XT(7)
+        GQ(1, 0)
+        G(1, 1, 0)
+        G(1, 1, 1)
+        G(1, 1, 2)
+        G(1, 1, 3)
+        XC(7)
+        GC(1, 1, 0)
+        GC(1, 1, 1)
+        GC(1, 1, 2)
+        GC(1, 1, 3)
+        XQ(1)
+        GI(0, 1)
+        PM(1, 0)
+        PM(1, 1)
+        GQ(0, 1)
+        GI(1, 1)
+        PC(1, 0)
+        PC(1, 1)
+        R(0, 0, 0)
+        R(0, 0, 1)
+        GQ(1, 1)
+        ST(0, 0, 0)
+        ST(0, 0, 1)
+        R(0, 1, 0)
+        R(0, 1, 1)
+        ST(0, 1, 0)
+        ST(0, 1, 1)
+        PM(1, 2)
+        PM(1, 3)
+        OT(0, 0, 1)
+        OT(0, 0, 0)
+        HR(0, 0)
+        PC(1, 2)
+        PC(1, 3)
+        OT(0, 1, 1)
+        OT(0, 1, 0)
+        HR(0, 1)
+        MM(0, 0)
+        MM(0, 1)
+        PM(1, 4)
+        PM(1, 5)
+        PI(1, 0)
+        R(1, 0, 0)
+        R(1, 0, 1)
+        R(1, 1, 0)
+        R(1, 1, 1)
+        PQ(1, 0)
+        PC(1, 4)
+        PC(1, 5)
+        ST(1, 0, 0)
+        ST(1, 0, 1)
+        ST(1, 1, 0)
+        ST(1, 1, 1)
+        PM(1, 6)
+        PM(1, 7)
+        OT(1, 0, 1)
+        OT(1, 0, 0)
+        HR(1, 0)
+        PC(1, 6)
+        PC(1, 7)
+        OT(1, 1, 1)
+        OT(1, 1, 0)
+        HR(1, 1)
+        MM(1, 0)
+        PI(1, 1)
+        MM(1, 1)
+        PQ(1, 1)
+        R(2, 0, 0)
+        ST(2, 0, 0, 'V')
+        R(2, 0, 1)
+        ST(2, 0, 1, 'V')
+        R(2, 1, 0)
+        ST(2, 1, 0, 'V')
+        R(2, 1, 1)
+        ST(2, 1, 1, 'V')
+        OT(2, 0, 1)
+        OT(2, 0, 0)
+        HR(2, 0)
+        MM(2, 0)
+        R(3, 0, 0)
+        ST(3, 0, 0, 'V')
+        R(3, 0, 1)
+        ST(3, 0, 1, 'V')
+        R(3, 1, 0)
+        ST(3, 1, 0, 'V')
+        R(3, 1, 1)
+        ST(3, 1, 1, 'V')
+        OT(2, 1, 1)
+        OT(2, 1, 0)
+        HR(2, 1)
+        MM(2, 1)
+        OT(3, 0, 1)
+        OT(3, 0, 0)
+        HR(3, 0)
+        OT(3, 1, 1)
+        OT(3, 1, 0)
+        HR(3, 1)
+        MM(3, 0)
+        MM(3, 1)

@@ -40,18 +40,30 @@ def tile_bjorckmaxmindense_kernel(tc, x_bytes, x_scale, w, d, s, t, b, out):
                 T[key] = tl
             return T[key]
 
+        TRS = [(1, 0, 1), (1, 0, 2), (1, 0, 3)]
         sc = const.tile([P, D], F32, align_bytes=64)
         d_sb = const.tile([P, KP, 4], BF16)
         nc.gpsimd.dma_start(out=d_sb[:], in_=d.rearrange("(g p j) -> p g j", p=P, j=4))
-        vec32 = []
+        rows = const.tile([P, 16, 8], BF16)
+        nc.gpsimd.memset(rows[:], 0.0)
         for i, v in enumerate((t, s, b)):
-            v16 = const.tile([P, CH, 4], BF16, name="v16_%d" % i)
-            nc.gpsimd.dma_start(out=v16[:], in_=v.rearrange("(c m t) -> m c t", m=P, t=4))
-            v32 = const.tile([P, CH, 4], F32, name="v32_%d" % i)
-            nc.gpsimd.tensor_copy(out=v32[:], in_=v16[:])
-            vec32.append(v32)
+            src = v.rearrange("(c a t b) -> c t a b", c=CH, a=16, t=4)
+            for c in range(CH):
+                r0 = 4 * (CH * i + c)
+                nc.gpsimd.dma_start(out=rows[r0 : r0 + 4], in_=src[c])
+        ident16 = const.tile([P, P], BF16)
+        make_identity(nc, ident16[:])
         ident = const.tile([P, P], F32)
         make_identity(nc, ident[:])
+        vec32 = const.tile([P, 3, CH, 4], F32)
+
+        def VEC():
+            vt = psum.tile([P, P], BF16, name="vt", tag="tr", bufs=3)
+            nc.tensor.transpose(vt[:], rows[:].rearrange("p a b -> p (a b)"), ident16[:])
+            nc.vector.tensor_copy(
+                out=vec32[:].rearrange("p i c t -> p (i c t)"), in_=vt[:, 0 : 12 * CH]
+            )
+
         wq = const.tile([P, KP, F], U32, align_bytes=64)
         wqs = const.tile([P, KP, F], U8, align_bytes=64)
         wdqs = const.tile([P, KP, F], U8, align_bytes=64)
@@ -79,12 +91,13 @@ def tile_bjorckmaxmindense_kernel(tc, x_bytes, x_scale, w, d, s, t, b, out):
             return big(("wg", kp), [P, CH, 4, P, 4], BF16, "g8", 5)
 
         def WI(kp, c, t0, n, e):
-            srcv = T["wr", kp][:].rearrange("p j (c m t) -> p c t m j", c=CH, t=4)
-            o, i = wg_of(kp)[:, c, t0 : t0 + n], srcv[:, c, t0 : t0 + n]
-            if e == "S":
-                nc.scalar.copy(out=o, in_=i)
-            else:
-                nc.vector.tensor_copy(out=o, in_=i)
+            srcv = T["wr", kp][:].rearrange("p j (c a t b) -> p c t a b j", c=CH, a=16, t=4)
+            for tt in range(t0, t0 + n):
+                o = wg_of(kp)[:, c, tt].rearrange("p (a b) j -> p a b j", a=16)
+                if e == "S":
+                    nc.scalar.copy(out=o, in_=srcv[:, c, tt])
+                else:
+                    nc.vector.tensor_copy(out=o, in_=srcv[:, c, tt])
 
         def WQ(kp):
             nc.vector.quantize_mx(
@@ -157,9 +170,9 @@ def tile_bjorckmaxmindense_kernel(tc, x_bytes, x_scale, w, d, s, t, b, out):
             acc = T["pa", h, ct]
             pl = big(("ppl", h, c), [P, 4, 512], BF16, "b4", 6)
             pb = big(("p15", h, c), [P, 4, 512], F32, "w8", 4)
-            nc.scalar.activation(out=pl[:, tt, :], in_=acc[:], func=ACT.Copy, scale=vec32[1][:, c, tt : tt + 1])
+            nc.scalar.activation(out=pl[:, tt, :], in_=acc[:], func=ACT.Copy, scale=vec32[:, 1, c, tt : tt + 1])
             nc.scalar.activation(
-                out=pb[:, tt, :], in_=acc[:], func=ACT.Identity, scale=1.5, bias=vec32[2][:, c, tt : tt + 1]
+                out=pb[:, tt, :], in_=acc[:], func=ACT.Identity, scale=1.5, bias=vec32[:, 2, c, tt : tt + 1]
             )
 
         def ILV(src, key, e):
@@ -179,7 +192,7 @@ def tile_bjorckmaxmindense_kernel(tc, x_bytes, x_scale, w, d, s, t, b, out):
             )
 
         def G(c, hh, tt, kps=range(KP)):
-            acc = bank(("ga", c, hh, tt), [P, 512], "acc", 5)
+            acc = bank(("ga", c, hh, tt), [P, 512], "tr", 3) if (c, hh, tt) in TRS else bank(("ga", c, hh, tt), [P, 512], "acc", 5)
             sl = slice(512 * c + P * tt, 512 * c + P * (tt + 1))
             cols = slice(512 * hh, 512 * (hh + 1))
             for kp in kps:
@@ -196,7 +209,7 @@ def tile_bjorckmaxmindense_kernel(tc, x_bytes, x_scale, w, d, s, t, b, out):
         def GC(c, hh, tt):
             pl = big(("gpl", c, hh), [P, 4, 512], BF16, "b4", 6)
             nc.scalar.activation(
-                out=pl[:, tt, :], in_=T["ga", c, hh, tt][:], func=ACT.Copy, scale=vec32[0][:, c, tt : tt + 1]
+                out=pl[:, tt, :], in_=T["ga", c, hh, tt][:], func=ACT.Copy, scale=vec32[:, 0, c, tt : tt + 1]
             )
 
         def GI(c, hh, e="V"):
@@ -234,7 +247,7 @@ def tile_bjorckmaxmindense_kernel(tc, x_bytes, x_scale, w, d, s, t, b, out):
             if e == "V":
                 nc.vector.scalar_tensor_tensor(out=o, in0=acc[:], scalar=-0.5, in1=p15, op0=ALU.mult, op1=ALU.add)
             else:
-                rs = big(("rs", q, c, tp), [P, 2, 256], F32, "hr", 3)
+                rs = big(("rs", q, c, tp), [P, 2, 256], F32, "hr", 2)
                 nc.scalar.activation(out=rs[:], in_=acc[:], func=ACT.Copy, scale=-0.5)
                 nc.gpsimd.tensor_tensor(out=o, in0=rs[:], in1=p15, op=ALU.add)
 
@@ -244,246 +257,245 @@ def tile_bjorckmaxmindense_kernel(tc, x_bytes, x_scale, w, d, s, t, b, out):
                 nc.tensor.transpose(bk[:, tt, :], T["ht", q, c][:, tt, P * i : P * (i + 1)], ident[:])
 
         def HR(q, i):
-            hr = big(("hr", q, i), [P, P, 4], F32, "hr", 2)
-            nc.scalar.copy(out=hr[:], in_=T["ot", q, i, 1][:].rearrange("p t m -> p m t"))
+            hr = big(("hr", q, i), [P, 16, 4, 8], F32, "hr", 2)
+            nc.scalar.copy(out=hr[:], in_=T["ot", q, i, 1][:].rearrange("p t (a b) -> p a t b", a=16))
 
         def MM(q, i):
             blk = 2 * q + i
-            o = big(("o", q, i), [P, 2, P, 4], F32, "b4", 6)
-            hl = T["ot", q, i, 0][:].rearrange("p t m -> p m t")
+            o = big(("o", q, i), [P, 2, 16, 4, 8], F32, "b4", 6)
+            hl = T["ot", q, i, 0][:].rearrange("p t (a b) -> p a t b", a=16)
             hr = T["hr", q, i]
             nc.vector.tensor_tensor(out=o[:, 0], in0=hl, in1=hr[:], op=ALU.max)
             nc.vector.tensor_tensor(out=o[:, 1], in0=hl, in1=hr[:], op=ALU.min)
-            nc.sync.dma_start(out=out[P * blk : P * (blk + 1), :], in_=o[:].rearrange("p c m t -> p (c m t)"))
+            nc.sync.dma_start(out=out[P * blk : P * (blk + 1), :], in_=o[:].rearrange("p c a t b -> p (c a t b)"))
 
+        ctx.enter_context(tc.manual_schedule())
         LW(0)
-        LSC()
-        LX(0)
-        LX(1)
         LW(1)
-        LX(2)
-        LX(3)
-        LW(2)
-        LW(3)
-        LX(4)
-        LX(5)
-        LX(6)
-        LX(7)
         WI(0, 0, 0, 4, "S")
         WI(0, 1, 0, 4, "V")
         WQ(0)
-        XP(0)
-        XT(0)
-        XP(1)
-        XT(1)
+        LSC()
         WI(1, 0, 0, 4, "S")
-        WI(1, 1, 0, 1, "V")
-        XC(0)
-        WI(1, 1, 1, 3, "S")
-        XC(1)
-        XP(2)
-        XT(2)
-        WQ(1)
-        WI(2, 0, 0, 4, "S")
-        WI(2, 1, 0, 1, "V")
-        WI(2, 1, 1, 3, "S")
-        XC(2)
-        XP(3)
-        XT(3)
-        WQ(2)
-        WI(3, 1, 0, 1, "V")
-        XC(3)
-        WI(3, 0, 0, 4, "S")
-        WI(3, 1, 1, 3, "S")
-        XQ(0)
-        PM(0, 0, [0])
-        PM(0, 1, [0])
-        PM(0, 2, [0])
-        PM(0, 3, [0])
-        PM(0, 4, [0])
-        PM(0, 0, [1])
-        PM(0, 1, [1])
-        PM(0, 2, [1])
-        PM(0, 3, [1])
-        PM(0, 4, [1])
-        PM(0, 0, [2])
-        PM(0, 1, [2])
-        PM(0, 2, [2])
-        PM(0, 3, [2])
-        PM(0, 4, [2])
         WD(0)
-        WQ(3)
+        WI(1, 1, 0, 1, "V")
+        WI(1, 1, 1, 3, "S")
+        LW(2)
+        LW(3)
+        WI(2, 0, 0, 4, "S")
+        LX(0)
         WDQ(0)
-        PM(0, 0, [3])
-        PM(0, 1, [3])
-        PM(0, 2, [3])
-        PM(0, 3, [3])
-        PM(0, 4, [3])
-        PC(0, 0)
-        PC(0, 1)
-        PC(0, 2)
-        PC(0, 3)
-        PC(0, 4)
-        PM(0, 5)
-        PC(0, 5)
-        PM(0, 6)
-        PC(0, 6)
-        PM(0, 7)
-        PC(0, 7)
         WD(1)
+        LX(1)
+        LX(2)
+        WI(2, 1, 0, 1, "V")
+        VEC()
+        WQ(1)
         WDQ(1)
+        LX(3)
+        WI(2, 1, 1, 3, "S")
+        G(0, 0, 1, (0,))
+        G(0, 0, 0, (0,))
+        G(1, 0, 0, (0,))
+        G(1, 0, 0, (1,))
+        G(0, 0, 3, (0,))
+        G(1, 0, 1, (0,))
+        WI(3, 1, 0, 1, "V")
+        WI(3, 0, 0, 4, "S")
         WD(2)
+        WQ(2)
+        G(0, 0, 3, (1,))
+        G(1, 0, 3, (0,))
         WDQ(2)
-        PI(0, 0)
+        WI(3, 1, 1, 3, "S")
+        G(1, 0, 2, (0,))
+        G(0, 0, 1, (1,))
+        G(1, 0, 3, (1,))
+        G(1, 0, 1, (1,))
         WD(3)
-        PQ(0, 0)
+        G(0, 0, 2, (0,))
+        G(1, 0, 1, (2,))
+        WQ(3)
         WDQ(3)
-        G(0, 0, 0, [0])
-        G(0, 0, 1, [0])
-        G(0, 0, 2, [0])
-        G(0, 0, 3, [0])
-        G(0, 0, 0, [1])
-        G(0, 0, 1, [1])
-        G(0, 0, 2, [1])
-        G(0, 0, 3, [1])
-        G(0, 0, 0, [2])
-        G(0, 0, 1, [2])
-        G(0, 0, 2, [2])
-        G(0, 0, 3, [2])
-        G(0, 0, 0, [3])
-        G(0, 0, 1, [3])
-        G(0, 0, 2, [3])
-        G(0, 0, 3, [3])
-        XP(4)
-        XT(4)
-        PI(0, 1)
-        XP(5)
-        PQ(0, 1)
-        XT(5)
+        G(0, 0, 2, (1,))
+        G(1, 0, 2, (1,))
+        G(0, 0, 0, (1,))
+        G(1, 0, 3, (2,))
+        G(1, 0, 2, (2,))
+        G(1, 0, 0, (2,))
+        G(0, 0, 1, (2,))
+        G(0, 0, 3, (2,))
+        G(0, 0, 0, (2,))
+        G(0, 0, 2, (2,))
+        G(1, 0, 0, (3,))
+        XP(1)
+        G(0, 0, 0, (3,))
         GC(0, 0, 0)
+        G(0, 0, 1, (3,))
+        G(0, 0, 3, (3,))
+        G(1, 0, 1, (3,))
+        G(1, 0, 3, (3,))
         GC(0, 0, 1)
-        GC(0, 0, 2)
-        GC(0, 0, 3)
-        G(1, 0, 0)
-        G(1, 0, 1)
-        G(1, 0, 2)
-        G(1, 0, 3)
-        XC(4)
-        XC(5)
-        GC(1, 0, 0)
-        GC(1, 0, 1)
-        GC(1, 0, 2)
-        GC(1, 0, 3)
-        GI(0, 0)
-        XP(6)
-        XT(6)
-        GQ(0, 0)
         G(0, 1, 0)
+        XP(0)
+        LX(4)
+        GC(1, 0, 1)
+        GC(1, 0, 3)
+        XT(1)
+        GC(0, 0, 3)
+        XC(1)
+        GC(1, 0, 0)
         G(0, 1, 1)
+        G(0, 0, 2, (3,))
+        LX(5)
+        GC(0, 0, 2)
+        XP(2)
+        XT(0)
+        XC(0)
+        G(1, 0, 2, (3,))
         G(0, 1, 2)
-        G(0, 1, 3)
-        XC(6)
-        GI(1, 0)
-        GC(0, 1, 0)
-        GC(0, 1, 1)
+        XP(3)
+        GC(1, 0, 2)
+        XT(2)
         GC(0, 1, 2)
-        GC(0, 1, 3)
-        XP(7)
-        XT(7)
-        GQ(1, 0)
-        G(1, 1, 0)
-        G(1, 1, 1)
-        G(1, 1, 2)
+        XC(2)
+        XT(3)
+        XP(4)
         G(1, 1, 3)
-        XC(7)
-        GC(1, 1, 0)
+        G(1, 1, 1)
+        XC(3)
+        GC(0, 1, 0)
+        XQ(0)
+        XP(5)
+        LX(6)
+        GI(1, 0, 'V')
+        GI(0, 0, 'V')
+        G(0, 1, 3)
         GC(1, 1, 1)
-        GC(1, 1, 2)
+        XT(4)
+        GC(0, 1, 1)
         GC(1, 1, 3)
-        XQ(1)
-        GI(0, 1)
-        PM(1, 0)
-        PM(1, 1)
+        PM(0, 1)
+        PM(0, 3)
+        XC(4)
+        PM(0, 2)
+        GC(0, 1, 3)
+        G(1, 1, 2)
+        PM(0, 0)
+        PC(0, 1)
+        XT(5)
+        PC(0, 2)
+        PM(0, 4)
+        PC(0, 3)
+        XP(6)
+        PC(0, 0)
+        LX(7)
+        GI(0, 1, 'V')
+        XC(5)
+        PC(0, 4)
+        XP(7)
+        PM(0, 5)
+        XT(6)
+        XC(6)
+        XT(7)
+        PM(0, 6)
+        PM(0, 7)
+        XC(7)
+        G(1, 1, 0)
         GQ(0, 1)
-        GI(1, 1)
+        GC(1, 1, 2)
+        PC(0, 5)
+        PI(0, 0, 'V')
+        PC(0, 6)
+        XQ(1)
+        PC(0, 7)
+        GQ(0, 0)
+        PM(1, 0)
+        PI(0, 1, 'V')
         PC(1, 0)
-        PC(1, 1)
-        R(0, 0, 0)
-        R(0, 0, 1)
-        GQ(1, 1)
-        ST(0, 0, 0)
-        ST(0, 0, 1)
-        R(0, 1, 0)
-        R(0, 1, 1)
-        ST(0, 1, 0)
-        ST(0, 1, 1)
+        PQ(0, 0)
         PM(1, 2)
         PM(1, 3)
-        OT(0, 0, 1)
-        OT(0, 0, 0)
-        HR(0, 0)
-        PC(1, 2)
+        PM(1, 1)
+        GC(1, 1, 0)
         PC(1, 3)
-        OT(0, 1, 1)
-        OT(0, 1, 0)
-        HR(0, 1)
-        MM(0, 0)
-        MM(0, 1)
-        PM(1, 4)
+        PQ(0, 1)
+        PC(1, 2)
+        GI(1, 1, 'V')
         PM(1, 5)
-        PI(1, 0)
-        R(1, 0, 0)
-        R(1, 0, 1)
+        GQ(1, 0)
+        R(0, 0, 0)
+        GQ(1, 1)
+        R(0, 0, 1)
         R(1, 1, 0)
-        R(1, 1, 1)
-        PQ(1, 0)
-        PC(1, 4)
+        PC(1, 1)
+        ST(0, 0, 1, 'V')
+        R(1, 0, 1)
+        R(0, 1, 1)
+        ST(1, 1, 0, 'V')
         PC(1, 5)
-        ST(1, 0, 0)
-        ST(1, 0, 1)
-        ST(1, 1, 0)
-        ST(1, 1, 1)
-        PM(1, 6)
+        R(0, 1, 0)
+        ST(1, 0, 1, 'V')
+        ST(0, 1, 0, 'V')
+        ST(0, 1, 1, 'V')
+        PI(1, 0, 'V')
         PM(1, 7)
-        OT(1, 0, 1)
-        OT(1, 0, 0)
-        HR(1, 0)
-        PC(1, 6)
+        PM(1, 4)
+        OT(0, 1, 1)
         PC(1, 7)
-        OT(1, 1, 1)
+        R(1, 1, 1)
+        ST(0, 0, 0, 'V')
+        PQ(1, 0)
+        R(1, 0, 0)
+        OT(0, 0, 1)
+        OT(0, 1, 0)
+        ST(1, 1, 1, 'V')
+        HR(0, 1)
+        HR(0, 0)
+        OT(0, 0, 0)
+        PC(1, 4)
+        PM(1, 6)
+        ST(1, 0, 0, 'V')
+        OT(1, 0, 0)
+        MM(0, 1)
+        OT(1, 0, 1)
+        PC(1, 6)
+        HR(1, 0)
         OT(1, 1, 0)
-        HR(1, 1)
-        MM(1, 0)
-        PI(1, 1)
-        MM(1, 1)
+        MM(0, 0)
+        PI(1, 1, 'V')
+        OT(1, 1, 1)
         PQ(1, 1)
-        R(2, 0, 0)
-        ST(2, 0, 0, 'V')
-        R(2, 0, 1)
-        ST(2, 0, 1, 'V')
-        R(2, 1, 0)
-        ST(2, 1, 0, 'V')
+        HR(1, 1)
         R(2, 1, 1)
+        R(2, 1, 0)
+        R(2, 0, 1)
+        MM(1, 0)
         ST(2, 1, 1, 'V')
-        OT(2, 0, 1)
-        OT(2, 0, 0)
-        HR(2, 0)
-        MM(2, 0)
+        ST(2, 1, 0, 'V')
         R(3, 0, 0)
-        ST(3, 0, 0, 'V')
-        R(3, 0, 1)
-        ST(3, 0, 1, 'V')
+        R(2, 0, 0)
         R(3, 1, 0)
-        ST(3, 1, 0, 'V')
         R(3, 1, 1)
-        ST(3, 1, 1, 'V')
         OT(2, 1, 1)
-        OT(2, 1, 0)
+        ST(2, 0, 1, 'V')
+        MM(1, 1)
+        OT(2, 0, 1)
+        ST(2, 0, 0, 'V')
         HR(2, 1)
+        ST(3, 0, 0, 'V')
+        OT(2, 1, 0)
+        HR(2, 0)
+        ST(3, 1, 1, 'V')
+        ST(3, 1, 0, 'V')
+        R(3, 0, 1)
+        OT(2, 0, 0)
         MM(2, 1)
         OT(3, 0, 1)
-        OT(3, 0, 0)
+        ST(3, 0, 1, 'V')
         HR(3, 0)
+        OT(3, 0, 0)
+        MM(2, 0)
         OT(3, 1, 1)
         OT(3, 1, 0)
         HR(3, 1)

@@ -40,17 +40,16 @@ def tile_bjorckmaxmindense_kernel(tc, x_bytes, x_scale, w, d, s, t, b, out):
                 T[key] = tl
             return T[key]
 
-        TRS = [(1, 0, 1), (1, 0, 2), (1, 0, 3)]
         sc = const.tile([P, D], F32, align_bytes=64)
         d_sb = const.tile([P, KP, 4], BF16)
-        nc.gpsimd.dma_start(out=d_sb[:], in_=d.rearrange("(g p j) -> p g j", p=P, j=4))
+        nc.scalar.dma_start(out=d_sb[:], in_=d.rearrange("(g p j) -> p g j", p=P, j=4))
         rows = const.tile([P, 16, 8], BF16)
-        nc.gpsimd.memset(rows[:], 0.0)
+        nc.vector.memset(rows[:], 0.0)
         for i, v in enumerate((t, s, b)):
             src = v.rearrange("(c a t b) -> c t a b", c=CH, a=16, t=4)
             for c in range(CH):
                 r0 = 4 * (CH * i + c)
-                nc.gpsimd.dma_start(out=rows[r0 : r0 + 4], in_=src[c])
+                nc.scalar.dma_start(out=rows[r0 : r0 + 4], in_=src[c])
         ident16 = const.tile([P, P], BF16)
         make_identity(nc, ident16[:])
         ident = const.tile([P, P], F32)
@@ -58,11 +57,9 @@ def tile_bjorckmaxmindense_kernel(tc, x_bytes, x_scale, w, d, s, t, b, out):
         vec32 = const.tile([P, 3, CH, 4], F32)
 
         def VEC():
-            vt = psum.tile([P, P], BF16, name="vt", tag="tr", bufs=3)
+            vt = psum.tile([P, P], BF16, name="vt", tag="bk", bufs=8)
             nc.tensor.transpose(vt[:], rows[:].rearrange("p a b -> p (a b)"), ident16[:])
-            nc.vector.tensor_copy(
-                out=vec32[:].rearrange("p i c t -> p (i c t)"), in_=vt[:, 0 : 12 * CH]
-            )
+            nc.scalar.copy(out=vec32[:].rearrange("p i c t -> p (i c t)"), in_=vt[:, 0 : 12 * CH])
 
         wq = const.tile([P, KP, F], U32, align_bytes=64)
         wqs = const.tile([P, KP, F], U8, align_bytes=64)
@@ -123,36 +120,32 @@ def tile_bjorckmaxmindense_kernel(tc, x_bytes, x_scale, w, d, s, t, b, out):
             xs = big(("xs", i), [P, D], BF16, "xs", 2)
             nc.vector.tensor_tensor(out=xs[:], in0=T["xb", i][:].bitcast(FP8), in1=sc[:], op=ALU.mult)
 
-        def XT(i):
+        def XT(i, g2):
             words = T["xs", i][:].bitcast(F32)
-            for g2 in range(2):
-                xt = bank(("xt", i, g2), [P, 2, 2, P], "tr", 3)
-                for gi in range(2):
-                    kp = 2 * g2 + gi
-                    for u in range(2):
-                        nc.tensor.transpose(xt[:, gi, u, :], words[:, 256 * kp + u : 256 * (kp + 1) : 2], ident[:])
+            xt = bank(("xt", i, g2), [P, 2, 2, P], "bk", 8)
+            for gi in range(2):
+                kp = 2 * g2 + gi
+                for u in range(2):
+                    nc.tensor.transpose(xt[:, gi, u, :], words[:, 256 * kp + u : 256 * (kp + 1) : 2], ident[:])
 
-        def XC(i):
+        def XC(i, g2):
             xg = big(("xg", i // 4), [P, KP, 512, 4], BF16, "xg", 2)
             r = P * (i % 4)
-            for g2 in range(2):
-                nc.scalar.copy(
-                    out=xg[:].bitcast(F32)[:, 2 * g2 : 2 * g2 + 2, r : r + P, :],
-                    in_=T["xt", i, g2][:].rearrange("p g u r -> p g r u"),
-                )
+            nc.scalar.copy(
+                out=xg[:].bitcast(F32)[:, 2 * g2 : 2 * g2 + 2, r : r + P, :],
+                in_=T["xt", i, g2][:].rearrange("p g u r -> p g r u"),
+            )
 
-        def XQ(h):
-            xg = T["xg", h]
-            for k2 in range(2):
-                ks = slice(2 * k2, 2 * k2 + 2)
-                nc.vector.quantize_mx(
-                    out=xq[:, h, ks, :].rearrange("p k n -> p (k n)").bitcast(FP8X4),
-                    scales=xqs[:, h, ks, :].rearrange("p k n -> p (k n)"),
-                    in_=xg[:, ks].rearrange("p k n t -> p (k n t)"),
-                )
+        def XQ(h, g2):
+            ks = slice(2 * g2, 2 * g2 + 2)
+            nc.vector.quantize_mx(
+                out=xq[:, h, ks, :].rearrange("p k n -> p (k n)").bitcast(FP8X4),
+                scales=xqs[:, h, ks, :].rearrange("p k n -> p (k n)"),
+                in_=T["xg", h][:, ks].rearrange("p k n t -> p (k n t)"),
+            )
 
         def PM(h, ct, kps=range(KP)):
-            acc = bank(("pa", h, ct), [P, 512], "acc", 5)
+            acc = bank(("pa", h, ct), [P, 512], "bk", 8)
             sl = slice(P * ct, P * (ct + 1))
             for kp in kps:
                 nc.tensor.matmul_mx(
@@ -192,7 +185,7 @@ def tile_bjorckmaxmindense_kernel(tc, x_bytes, x_scale, w, d, s, t, b, out):
             )
 
         def G(c, hh, tt, kps=range(KP)):
-            acc = bank(("ga", c, hh, tt), [P, 512], "tr", 3) if (c, hh, tt) in TRS else bank(("ga", c, hh, tt), [P, 512], "acc", 5)
+            acc = bank(("ga", c, hh, tt), [P, 512], "bk", 8)
             sl = slice(512 * c + P * tt, 512 * c + P * (tt + 1))
             cols = slice(512 * hh, 512 * (hh + 1))
             for kp in kps:
@@ -222,7 +215,7 @@ def tile_bjorckmaxmindense_kernel(tc, x_bytes, x_scale, w, d, s, t, b, out):
             )
 
         def R(q, c, tp):
-            acc = bank(("ra", q, c, tp), [P, 2, 256], "acc", 5)
+            acc = bank(("ra", q, c, tp), [P, 2, 256], "bk", 8)
             tok = slice(256 * q, 256 * (q + 1))
             for ti in range(2):
                 tt = 2 * tp + ti
@@ -247,12 +240,12 @@ def tile_bjorckmaxmindense_kernel(tc, x_bytes, x_scale, w, d, s, t, b, out):
             if e == "V":
                 nc.vector.scalar_tensor_tensor(out=o, in0=acc[:], scalar=-0.5, in1=p15, op0=ALU.mult, op1=ALU.add)
             else:
-                rs = big(("rs", q, c, tp), [P, 2, 256], F32, "hr", 2)
+                rs = big(("rs", q, c, tp), [P, 2, 256], F32, "xs", 2)
                 nc.scalar.activation(out=rs[:], in_=acc[:], func=ACT.Copy, scale=-0.5)
                 nc.gpsimd.tensor_tensor(out=o, in0=rs[:], in1=p15, op=ALU.add)
 
         def OT(q, i, c):
-            bk = bank(("ot", q, i, c), [P, 4, P], "tr", 3)
+            bk = bank(("ot", q, i, c), [P, 4, P], "bk", 8)
             for tt in range(4):
                 nc.tensor.transpose(bk[:, tt, :], T["ht", q, c][:, tt, P * i : P * (i + 1)], ident[:])
 
@@ -271,233 +264,272 @@ def tile_bjorckmaxmindense_kernel(tc, x_bytes, x_scale, w, d, s, t, b, out):
 
         ctx.enter_context(tc.manual_schedule())
         LW(0)
+        WI(0, 0, 0, 1, "S")
+        WI(0, 0, 1, 1, "V")
+        WI(0, 1, 0, 1, "S")
+        WI(0, 0, 2, 1, "V")
         LW(1)
-        WI(0, 0, 0, 4, "S")
-        WI(0, 1, 0, 4, "V")
-        WQ(0)
-        LSC()
-        WI(1, 0, 0, 4, "S")
-        WD(0)
-        WI(1, 1, 0, 1, "V")
-        WI(1, 1, 1, 3, "S")
         LW(2)
+        WI(0, 0, 3, 1, "V")
+        WI(1, 0, 0, 1, "S")
+        WI(1, 0, 1, 1, "S")
+        WI(0, 1, 1, 1, "V")
+        WI(1, 1, 0, 1, "S")
+        WI(0, 1, 2, 1, "V")
+        WI(1, 1, 1, 1, "S")
+        WI(0, 1, 3, 1, "V")
+        WI(1, 0, 2, 1, "V")
+        WI(1, 1, 2, 1, "S")
+        WQ(0)
         LW(3)
-        WI(2, 0, 0, 4, "S")
-        LX(0)
+        WI(1, 0, 3, 1, "S")
+        WI(2, 1, 0, 1, "S")
+        WI(2, 0, 0, 1, "S")
+        WD(0)
+        WI(1, 1, 3, 1, "V")
         WDQ(0)
-        WD(1)
         LX(1)
-        LX(2)
-        WI(2, 1, 0, 1, "V")
+        WI(2, 1, 1, 1, "S")
+        WI(2, 0, 1, 1, "V")
+        WD(1)
+        WI(3, 1, 0, 1, "S")
+        WI(2, 1, 2, 1, "S")
         VEC()
-        WQ(1)
-        WDQ(1)
-        LX(3)
-        WI(2, 1, 1, 3, "S")
-        G(0, 0, 1, (0,))
-        G(0, 0, 0, (0,))
-        G(1, 0, 0, (0,))
-        G(1, 0, 0, (1,))
-        G(0, 0, 3, (0,))
-        G(1, 0, 1, (0,))
-        WI(3, 1, 0, 1, "V")
-        WI(3, 0, 0, 4, "S")
-        WD(2)
-        WQ(2)
-        G(0, 0, 3, (1,))
-        G(1, 0, 3, (0,))
-        WDQ(2)
-        WI(3, 1, 1, 3, "S")
-        G(1, 0, 2, (0,))
-        G(0, 0, 1, (1,))
-        G(1, 0, 3, (1,))
-        G(1, 0, 1, (1,))
-        WD(3)
         G(0, 0, 2, (0,))
-        G(1, 0, 1, (2,))
-        WQ(3)
-        WDQ(3)
+        LX(3)
+        WQ(1)
+        G(0, 0, 1, (0,))
+        LX(4)
+        WDQ(1)
+        WI(2, 0, 2, 1, "S")
+        WI(2, 1, 3, 1, "S")
+        G(1, 0, 1, (0,))
+        G(0, 0, 3, (0,))
+        WI(2, 0, 3, 1, "S")
+        WD(2)
+        G(1, 0, 2, (0,))
+        WI(3, 1, 1, 1, "S")
+        G(0, 0, 1, (1,))
+        WQ(2)
+        G(1, 0, 0, (0,))
+        WI(3, 1, 2, 1, "S")
+        G(0, 0, 3, (1,))
+        WI(3, 0, 0, 1, "V")
+        WI(3, 0, 1, 1, "S")
+        WI(3, 0, 2, 1, "S")
         G(0, 0, 2, (1,))
+        WDQ(2)
+        G(1, 0, 1, (1,))
+        WI(3, 1, 3, 1, "S")
         G(1, 0, 2, (1,))
-        G(0, 0, 0, (1,))
-        G(1, 0, 3, (2,))
-        G(1, 0, 2, (2,))
-        G(1, 0, 0, (2,))
+        G(1, 0, 3, (0,))
+        LSC()
+        G(0, 0, 0, (0,))
         G(0, 0, 1, (2,))
-        G(0, 0, 3, (2,))
+        G(1, 0, 2, (2,))
+        WI(3, 0, 3, 1, "S")
+        G(1, 0, 1, (2,))
+        G(1, 0, 0, (1,))
+        WD(3)
+        G(0, 0, 0, (1,))
+        WQ(3)
+        G(1, 0, 3, (1,))
+        WDQ(3)
+        G(1, 0, 0, (2,))
         G(0, 0, 0, (2,))
-        G(0, 0, 2, (2,))
-        G(1, 0, 0, (3,))
-        XP(1)
+        G(1, 0, 3, (2,))
+        G(0, 0, 3, (2,))
+        G(1, 0, 1, (3,))
         G(0, 0, 0, (3,))
         GC(0, 0, 0)
-        G(0, 0, 1, (3,))
-        G(0, 0, 3, (3,))
-        G(1, 0, 1, (3,))
         G(1, 0, 3, (3,))
-        GC(0, 0, 1)
-        G(0, 1, 0)
-        XP(0)
-        LX(4)
-        GC(1, 0, 1)
-        GC(1, 0, 3)
-        XT(1)
-        GC(0, 0, 3)
-        XC(1)
-        GC(1, 0, 0)
-        G(0, 1, 1)
-        G(0, 0, 2, (3,))
-        LX(5)
-        GC(0, 0, 2)
-        XP(2)
-        XT(0)
-        XC(0)
+        LX(0)
         G(1, 0, 2, (3,))
-        G(0, 1, 2)
-        XP(3)
+        XP(0)
+        G(0, 0, 3, (3,))
+        G(0, 0, 2, (2,))
+        GC(0, 0, 3)
         GC(1, 0, 2)
-        XT(2)
-        GC(0, 1, 2)
-        XC(2)
-        XT(3)
-        XP(4)
-        G(1, 1, 3)
-        G(1, 1, 1)
-        XC(3)
-        GC(0, 1, 0)
-        XQ(0)
-        XP(5)
-        LX(6)
-        GI(1, 0, 'V')
-        GI(0, 0, 'V')
-        G(0, 1, 3)
-        GC(1, 1, 1)
-        XT(4)
-        GC(0, 1, 1)
-        GC(1, 1, 3)
-        PM(0, 1)
-        PM(0, 3)
-        XC(4)
-        PM(0, 2)
-        GC(0, 1, 3)
-        G(1, 1, 2)
-        PM(0, 0)
-        PC(0, 1)
-        XT(5)
-        PC(0, 2)
-        PM(0, 4)
-        PC(0, 3)
-        XP(6)
-        PC(0, 0)
+        G(0, 0, 1, (3,))
+        GC(1, 0, 3)
+        LX(2)
+        G(1, 0, 0, (3,))
+        GC(1, 0, 0)
+        G(0, 1, 2)
+        XP(1)
         LX(7)
-        GI(0, 1, 'V')
-        XC(5)
-        PC(0, 4)
-        XP(7)
-        PM(0, 5)
-        XT(6)
-        XC(6)
-        XT(7)
-        PM(0, 6)
-        PM(0, 7)
-        XC(7)
+        XT(0, 1)
+        GC(1, 0, 1)
+        XT(0, 0)
+        XC(0, 0)
+        XT(1, 0)
+        G(0, 0, 2, (3,))
+        XP(3)
+        XC(1, 0)
+        G(1, 1, 2)
+        XT(1, 1)
+        XP(2)
+        XT(3, 1)
+        XT(3, 0)
+        LX(5)
+        XC(0, 1)
+        G(0, 1, 3)
+        GC(0, 0, 1)
+        GC(0, 1, 3)
+        XC(3, 0)
+        G(0, 1, 1)
+        XP(5)
+        XT(2, 0)
+        XT(2, 1)
+        GC(0, 1, 2)
         G(1, 1, 0)
-        GQ(0, 1)
+        LX(6)
+        XP(4)
+        GC(0, 0, 2)
+        G(1, 1, 1)
+        XC(2, 0)
+        XC(1, 1)
+        XC(2, 1)
+        XQ(0, 0)
+        XT(5, 1)
+        XT(5, 0)
+        XT(4, 1)
+        XC(3, 1)
+        GC(1, 1, 0)
+        XQ(0, 1)
+        XC(4, 1)
+        XT(4, 0)
+        PM(0, 3)
+        XC(4, 0)
+        PM(0, 2)
+        XC(5, 1)
+        PM(0, 1)
+        PM(0, 7)
+        XP(7)
+        XP(6)
+        PC(0, 3)
+        GC(1, 1, 1)
+        PM(0, 0)
+        PC(0, 2)
+        XT(6, 0)
         GC(1, 1, 2)
-        PC(0, 5)
+        XT(7, 1)
+        PC(0, 1)
+        XT(6, 1)
+        GC(0, 1, 1)
+        XT(7, 0)
+        GI(0, 0, 'V')
+        XC(5, 0)
+        XC(6, 1)
+        PM(0, 4)
+        G(0, 1, 0)
+        PM(0, 6)
+        XC(7, 0)
+        PM(0, 5)
+        GI(1, 0, 'V')
+        XC(7, 1)
+        G(1, 1, 3)
+        XC(6, 0)
+        GQ(0, 0)
+        XQ(1, 1)
+        XQ(1, 0)
+        PC(0, 4)
+        PC(0, 0)
+        PC(0, 7)
+        GC(0, 1, 0)
+        PM(1, 4)
         PI(0, 0, 'V')
         PC(0, 6)
-        XQ(1)
-        PC(0, 7)
-        GQ(0, 0)
-        PM(1, 0)
-        PI(0, 1, 'V')
-        PC(1, 0)
-        PQ(0, 0)
-        PM(1, 2)
-        PM(1, 3)
-        PM(1, 1)
-        GC(1, 1, 0)
-        PC(1, 3)
-        PQ(0, 1)
-        PC(1, 2)
-        GI(1, 1, 'V')
-        PM(1, 5)
+        PC(0, 5)
         GQ(1, 0)
-        R(0, 0, 0)
-        GQ(1, 1)
-        R(0, 0, 1)
-        R(1, 1, 0)
+        PM(1, 5)
+        PM(1, 1)
+        PQ(0, 0)
+        GI(0, 1, 'V')
+        GC(1, 1, 3)
         PC(1, 1)
-        ST(0, 0, 1, 'V')
-        R(1, 0, 1)
-        R(0, 1, 1)
-        ST(1, 1, 0, 'V')
-        PC(1, 5)
-        R(0, 1, 0)
-        ST(1, 0, 1, 'V')
-        ST(0, 1, 0, 'V')
-        ST(0, 1, 1, 'V')
-        PI(1, 0, 'V')
-        PM(1, 7)
-        PM(1, 4)
-        OT(0, 1, 1)
-        PC(1, 7)
-        R(1, 1, 1)
-        ST(0, 0, 0, 'V')
-        PQ(1, 0)
-        R(1, 0, 0)
-        OT(0, 0, 1)
-        OT(0, 1, 0)
-        ST(1, 1, 1, 'V')
-        HR(0, 1)
-        HR(0, 0)
-        OT(0, 0, 0)
+        PM(1, 3)
+        PI(0, 1, 'V')
         PC(1, 4)
+        GQ(0, 1)
+        PQ(0, 1)
+        PM(1, 7)
+        PC(1, 5)
+        GI(1, 1, 'V')
+        GQ(1, 1)
         PM(1, 6)
-        ST(1, 0, 0, 'V')
-        OT(1, 0, 0)
-        MM(0, 1)
-        OT(1, 0, 1)
+        PC(1, 3)
+        PC(1, 7)
+        R(0, 0, 0)
+        R(0, 0, 1)
+        R(0, 1, 0)
+        ST(0, 0, 0, 'V')
+        R(0, 1, 1)
+        ST(0, 1, 0, 'V')
+        ST(0, 0, 1, 'V')
         PC(1, 6)
-        HR(1, 0)
-        OT(1, 1, 0)
-        MM(0, 0)
+        PM(1, 2)
+        PM(1, 0)
+        ST(0, 1, 1, 'V')
+        PC(1, 2)
+        R(1, 0, 1)
+        R(1, 0, 0)
         PI(1, 1, 'V')
-        OT(1, 1, 1)
         PQ(1, 1)
-        HR(1, 1)
-        R(2, 1, 1)
+        PC(1, 0)
+        PI(1, 0, 'V')
+        OT(0, 1, 1)
+        OT(0, 1, 0)
+        OT(0, 0, 1)
+        PQ(1, 0)
+        OT(0, 0, 0)
+        ST(1, 0, 0, 'G')
+        R(1, 1, 0)
+        R(1, 1, 1)
+        ST(1, 0, 1, 'V')
+        HR(0, 1)
+        MM(0, 1)
+        R(3, 0, 1)
+        ST(1, 1, 1, 'G')
+        ST(1, 1, 0, 'V')
+        R(2, 0, 0)
         R(2, 1, 0)
         R(2, 0, 1)
-        MM(1, 0)
-        ST(2, 1, 1, 'V')
-        ST(2, 1, 0, 'V')
+        HR(0, 0)
+        R(2, 1, 1)
+        OT(1, 0, 1)
+        ST(2, 1, 0, 'G')
+        OT(1, 0, 0)
+        MM(0, 0)
+        ST(3, 0, 1, 'V')
+        OT(1, 1, 1)
+        ST(2, 0, 0, 'G')
+        HR(1, 0)
+        HR(1, 1)
+        OT(1, 1, 0)
         R(3, 0, 0)
-        R(2, 0, 0)
+        ST(2, 1, 1, 'V')
+        MM(1, 0)
+        OT(2, 0, 1)
         R(3, 1, 0)
+        MM(1, 1)
+        ST(2, 0, 1, 'G')
         R(3, 1, 1)
         OT(2, 1, 1)
-        ST(2, 0, 1, 'V')
-        MM(1, 1)
-        OT(2, 0, 1)
-        ST(2, 0, 0, 'V')
-        HR(2, 1)
         ST(3, 0, 0, 'V')
-        OT(2, 1, 0)
         HR(2, 0)
+        ST(3, 1, 0, 'G')
         ST(3, 1, 1, 'V')
-        ST(3, 1, 0, 'V')
-        R(3, 0, 1)
         OT(2, 0, 0)
-        MM(2, 1)
-        OT(3, 0, 1)
-        ST(3, 0, 1, 'V')
-        HR(3, 0)
         OT(3, 0, 0)
+        OT(2, 1, 0)
         MM(2, 0)
+        HR(2, 1)
         OT(3, 1, 1)
         OT(3, 1, 0)
+        OT(3, 0, 1)
         HR(3, 1)
-        MM(3, 0)
+        MM(2, 1)
+        HR(3, 0)
         MM(3, 1)
+        MM(3, 0)

@@ -14,522 +14,463 @@ ACT = mybir.ActivationFunctionType
 
 P = 128
 N, D, F = 1024, 2048, 1024
-KP = D // 512
-CH = F // 512
+K_PASS = 512
+PASSES = D // K_PASS
+CHUNK = 512
+CHUNKS = F // CHUNK
+A, MEM, E = 16, 4, 8
+HALF = 512
+QUARTER = 256
 FLOPS = 2 * N * D * F + 2 * D * F * F + 2 * N * F * F
+
+VECTOR_PIECES = (
+    ((0, 0), (0, 2), (0, 3), (1, 0), (1, 2), (1, 3)),
+    ((0, 1), (0, 3)),
+    ((1, 0),),
+    ((0, 1),),
+)
+GPSIMD_SHARE = ((0, 0, 0), (1, 0, 0), (2, 0, 0), (3, 0, 0), (3, 0, 1), (3, 1, 0))
 
 
 def tile_bjorckmaxmindense_kernel(tc, x_bytes, x_scale, w, d, s, t, b, out):
     nc = tc.nc
     with ExitStack() as ctx:
-        const = ctx.enter_context(tc.tile_pool(name="const", bufs=1))
+        keep = ctx.enter_context(tc.tile_pool(name="keep", bufs=1))
         pool = ctx.enter_context(tc.tile_pool(name="pool", bufs=2))
         psum = ctx.enter_context(tc.psum_pool(name="psum", bufs=1))
+        tiles = {}
 
-        T = {}
+        def sbuf(key, shape, dtype, tag, bufs):
+            if key not in tiles:
+                tile = pool.tile(shape, dtype, name=tag, tag=tag, bufs=bufs, align_bytes=64)
+                tiles[key] = tile
+            return tiles[key]
 
-        def big(key, shape, dt, tag, bufs):
-            if key not in T:
-                tl = pool.tile(shape, dt, name=tag, tag=tag, bufs=bufs, align_bytes=64)
-                T[key] = tl
-            return T[key]
+        def bank(key, shape, dtype=F32):
+            if key not in tiles:
+                tile = psum.tile(shape, dtype, name="bank", tag="bank", bufs=8)
+                tiles[key] = tile
+            return tiles[key]
 
-        def bank(key, shape, tag, bufs, dt=F32):
-            if key not in T:
-                tl = psum.tile(shape, dt, name=tag, tag=tag, bufs=bufs)
-                T[key] = tl
-            return T[key]
+        wq = keep.tile([P, PASSES, F], U32, align_bytes=64)
+        wq_scales = keep.tile([P, PASSES, F], U8, align_bytes=64)
+        wdq_scales = keep.tile([P, PASSES, F], U8, align_bytes=64)
+        xq = keep.tile([P, 2, PASSES, HALF], U32, align_bytes=64)
+        xq_scales = keep.tile([P, 2, PASSES, HALF], U8, align_bytes=64)
+        gtq = keep.tile([P, CHUNKS, F], U32, align_bytes=64)
+        gtq_scales = keep.tile([P, CHUNKS, F], U8, align_bytes=64)
+        psq = keep.tile([P, CHUNKS, N], U32, align_bytes=64)
+        psq_scales = keep.tile([P, CHUNKS, N], U8, align_bytes=64)
 
-        sc = const.tile([P, D], F32, align_bytes=64)
-        d_sb = const.tile([P, KP, 4], BF16)
-        nc.scalar.dma_start(out=d_sb[:], in_=d.rearrange("(g p j) -> p g j", p=P, j=4))
-        rows = const.tile([P, 16, 8], BF16)
-        nc.vector.memset(rows[:], 0.0)
-        for i, v in enumerate((t, s, b)):
-            src = v.rearrange("(c a t b) -> c t a b", c=CH, a=16, t=4)
-            for c in range(CH):
-                r0 = 4 * (CH * i + c)
-                nc.scalar.dma_start(out=rows[r0 : r0 + 4], in_=src[c])
-        ident16 = const.tile([P, P], BF16)
+        x_scale_all = keep.tile([P, D], F32, align_bytes=64)
+        d_sb = keep.tile([P, PASSES, 4], BF16)
+        gain_rows = keep.tile([P, A, E], BF16)
+        gains = keep.tile([P, 3, CHUNKS, MEM], F32)
+        ident16 = keep.tile([P, P], BF16)
+        ident = keep.tile([P, P], F32)
+
+        nc.vector.memset(gain_rows[:], 0.0)
+        nc.gpsimd.dma_start(out=d_sb[:], in_=d.rearrange("(k p j) -> p k j", p=P, j=4))
         make_identity(nc, ident16[:])
-        ident = const.tile([P, P], F32)
         make_identity(nc, ident[:])
-        vec32 = const.tile([P, 3, CH, 4], F32)
 
-        def VEC():
-            vt = psum.tile([P, P], BF16, name="vt", tag="bk", bufs=8)
-            nc.tensor.transpose(vt[:], rows[:].rearrange("p a b -> p (a b)"), ident16[:])
-            nc.scalar.copy(out=vec32[:].rearrange("p i c t -> p (i c t)"), in_=vt[:, 0 : 12 * CH])
 
-        wq = const.tile([P, KP, F], U32, align_bytes=64)
-        wqs = const.tile([P, KP, F], U8, align_bytes=64)
-        wdqs = const.tile([P, KP, F], U8, align_bytes=64)
-        xq = const.tile([P, 2, KP, 512], U32, align_bytes=64)
-        xqs = const.tile([P, 2, KP, 512], U8, align_bytes=64)
-        gtq = const.tile([P, CH, F], U32, align_bytes=64)
-        gtqs = const.tile([P, CH, F], U8, align_bytes=64)
-        psq = const.tile([P, CH, N], U32, align_bytes=64)
-        psqs = const.tile([P, CH, N], U8, align_bytes=64)
+        def load_w(k):
+            raw = sbuf(("w raw", k), [P, 4, F], BF16, "eight_kib", 4)
+            rows = w[K_PASS * k : K_PASS * (k + 1), :].rearrange("(p j) f -> p j f", j=4)
+            if k < 2:
+                for c in range(CHUNKS):
+                    cols = slice(CHUNK * c, CHUNK * (c + 1))
+                    nc.sync.dma_start(out=raw[:, :, cols], in_=rows[:, :, cols])
+            else:
+                nc.sync.dma_start(out=raw[:], in_=rows)
 
-        def LW(kp):
-            w_raw = big(("wr", kp), [P, 4, F], BF16, "w8", 4)
-            src = w[512 * kp : 512 * (kp + 1), :].rearrange("(p j) f -> p j f", j=4)
-            for c in range(CH):
-                nc.sync.dma_start(out=w_raw[:, :, 512 * c : 512 * (c + 1)], in_=src[:, :, 512 * c : 512 * (c + 1)])
+        def load_x(i):
+            codes = sbuf(("x bytes", i), [P, D], U8, "x_bytes", 4)
+            nc.sync.dma_start(out=codes[:], in_=x_bytes[P * i : P * (i + 1), :])
 
-        def LX(i):
-            xb = big(("xb", i), [P, D], U8, "xb", 4)
-            nc.sync.dma_start(out=xb[:], in_=x_bytes[P * i : P * (i + 1), :])
+        def load_x_scale():
+            nc.sync.dma_start(out=x_scale_all[:], in_=x_scale.rearrange("o k -> (o k)").partition_broadcast(P))
 
-        def LSC():
-            nc.sync.dma_start(out=sc[:], in_=x_scale.rearrange("o k -> (o k)").partition_broadcast(P))
+        def load_gains():
+            for i, v in enumerate((t, s, b)):
+                rows = v.rearrange("(c a m e) -> c m a e", c=CHUNKS, a=A, m=MEM)
+                for c in range(CHUNKS):
+                    r0 = MEM * (CHUNKS * i + c)
+                    nc.scalar.dma_start(out=gain_rows[r0 : r0 + MEM], in_=rows[c])
 
-        def wg_of(kp):
-            return big(("wg", kp), [P, CH, 4, P, 4], BF16, "g8", 5)
+        def turn_gains():
+            turned = bank("gains", [P, P], BF16)
+            nc.tensor.transpose(turned[:], gain_rows[:].rearrange("p a e -> p (a e)"), ident16[:])
+            nc.scalar.copy(out=gains[:].rearrange("p i c m -> p (i c m)"), in_=turned[:, 0 : 3 * CHUNKS * MEM])
 
-        def WI(kp, c, t0, n, e):
-            srcv = T["wr", kp][:].rearrange("p j (c a t b) -> p c t a b j", c=CH, a=16, t=4)
-            for tt in range(t0, t0 + n):
-                o = wg_of(kp)[:, c, tt].rearrange("p (a b) j -> p a b j", a=16)
-                if e == "S":
-                    nc.scalar.copy(out=o, in_=srcv[:, c, tt])
-                else:
-                    nc.vector.tensor_copy(out=o, in_=srcv[:, c, tt])
 
-        def WQ(kp):
+        def grouped_w(k):
+            return sbuf(("w grouped", k), [P, CHUNKS, MEM, P, 4], BF16, "grouped", 5)
+
+        def interleave_w(k):
+            src = tiles["w raw", k][:].rearrange("p j (c a m e) -> p c m a e j", c=CHUNKS, a=A, m=MEM)
+            for c in range(CHUNKS):
+                for m in range(MEM):
+                    dst = grouped_w(k)[:, c, m].rearrange("p (a e) j -> p a e j", a=A)
+                    if (c, m) in VECTOR_PIECES[k]:
+                        nc.vector.tensor_copy(out=dst, in_=src[:, c, m])
+                    else:
+                        nc.scalar.copy(out=dst, in_=src[:, c, m])
+
+        def quantise_w(k):
             nc.vector.quantize_mx(
-                out=wq[:, kp, :].bitcast(FP8X4), scales=wqs[:, kp, :], in_=wg_of(kp)[:].rearrange("p c t m j -> p (c t m j)")
+                out=wq[:, k, :].bitcast(FP8X4),
+                scales=wq_scales[:, k, :],
+                in_=grouped_w(k)[:].rearrange("p c m q j -> p (c m q j)"),
             )
 
-        def WD(kp):
-            wdg = big(("wdg", kp), [P, F, 4], BF16, "g8", 5)
+        def make_wd(k):
+            wd = sbuf(("wd", k), [P, F, 4], BF16, "grouped", 5)
             nc.vector.tensor_tensor(
-                out=wdg[:],
-                in0=wg_of(kp)[:].rearrange("p c t m j -> p (c t m) j"),
-                in1=d_sb[:, kp : kp + 1, :].to_broadcast([P, F, 4]),
+                out=wd[:],
+                in0=grouped_w(k)[:].rearrange("p c m q j -> p (c m q) j"),
+                in1=d_sb[:, k : k + 1, :].to_broadcast([P, F, 4]),
                 op=ALU.mult,
             )
 
-        def WDQ(kp):
-            dq = big(("wdq", kp), [P, F], U32, "wdq", 4)
+        def quantise_wd(k):
+            codes = sbuf(("wd codes", k), [P, F], U32, "four_kib", 4)
             nc.vector.quantize_mx(
-                out=dq[:].bitcast(FP8X4), scales=wdqs[:, kp, :], in_=T["wdg", kp][:].rearrange("p f j -> p (f j)")
+                out=codes[:].bitcast(FP8X4),
+                scales=wdq_scales[:, k, :],
+                in_=tiles["wd", k][:].rearrange("p f j -> p (f j)"),
             )
 
-        def XP(i):
-            xs = big(("xs", i), [P, D], BF16, "xs", 2)
-            nc.vector.tensor_tensor(out=xs[:], in0=T["xb", i][:].bitcast(FP8), in1=sc[:], op=ALU.mult)
 
-        def XT(i, g2):
-            words = T["xs", i][:].bitcast(F32)
-            xt = bank(("xt", i, g2), [P, 2, 2, P], "bk", 8)
-            for gi in range(2):
-                kp = 2 * g2 + gi
-                for u in range(2):
-                    nc.tensor.transpose(xt[:, gi, u, :], words[:, 256 * kp + u : 256 * (kp + 1) : 2], ident[:])
-
-        def XC(i, g2):
-            xg = big(("xg", i // 4), [P, KP, 512, 4], BF16, "xg", 2)
-            r = P * (i % 4)
-            nc.scalar.copy(
-                out=xg[:].bitcast(F32)[:, 2 * g2 : 2 * g2 + 2, r : r + P, :],
-                in_=T["xt", i, g2][:].rearrange("p g u r -> p g r u"),
-            )
-
-        def XQ(h, g2):
-            ks = slice(2 * g2, 2 * g2 + 2)
-            nc.vector.quantize_mx(
-                out=xq[:, h, ks, :].rearrange("p k n -> p (k n)").bitcast(FP8X4),
-                scales=xqs[:, h, ks, :].rearrange("p k n -> p (k n)"),
-                in_=T["xg", h][:, ks].rearrange("p k n t -> p (k n t)"),
-            )
-
-        def PM(h, ct, kps=range(KP)):
-            acc = bank(("pa", h, ct), [P, 512], "bk", 8)
-            sl = slice(P * ct, P * (ct + 1))
-            for kp in kps:
+        def g_matmuls(c, n, m, passes):
+            acc = bank(("g", c, n, m), [P, CHUNK])
+            rows = slice(CHUNK * c + P * m, CHUNK * c + P * (m + 1))
+            cols = slice(CHUNK * n, CHUNK * (n + 1))
+            for k in passes:
                 nc.tensor.matmul_mx(
                     out=acc[:],
-                    lhsT=wq[:, kp, sl].bitcast(FP8X4),
-                    lhsT_scale=wqs[:, kp, sl],
-                    rhs=xq[:, h, kp, :].bitcast(FP8X4),
-                    rhs_scale=xqs[:, h, kp, :],
-                    start=(kp == 0),
-                    stop=(kp == KP - 1),
+                    lhsT=tiles["wd codes", k][:, rows].bitcast(FP8X4),
+                    lhsT_scale=wdq_scales[:, k, rows],
+                    rhs=wq[:, k, cols].bitcast(FP8X4),
+                    rhs_scale=wq_scales[:, k, cols],
+                    start=(k == 0),
+                    stop=(k == PASSES - 1),
                 )
 
-        def PC(h, ct):
-            c, tt = ct // 4, ct % 4
-            acc = T["pa", h, ct]
-            pl = big(("ppl", h, c), [P, 4, 512], BF16, "b4", 6)
-            pb = big(("p15", h, c), [P, 4, 512], F32, "w8", 4)
-            nc.scalar.activation(out=pl[:, tt, :], in_=acc[:], func=ACT.Copy, scale=vec32[:, 1, c, tt : tt + 1])
-            nc.scalar.activation(
-                out=pb[:, tt, :], in_=acc[:], func=ACT.Identity, scale=1.5, bias=vec32[:, 2, c, tt : tt + 1]
-            )
+        def g_sweep(k):
+            for c in range(CHUNKS):
+                for m in range(MEM):
+                    g_matmuls(c, 0, m, (k,))
 
-        def ILV(src, key, e):
-            gg = big(key, [P, 512, 4], BF16, "b4", 6)
-            if e == "S":
-                nc.scalar.copy(out=gg[:], in_=src[:].rearrange("p t n -> p n t"))
+        def g_pair(c, i):
+            for m in (2 * i, 2 * i + 1):
+                g_matmuls(c, 1, m, range(PASSES))
+
+        def gt_out(c, n, members):
+            planes = sbuf(("gt planes", c, n), [P, MEM, CHUNK], BF16, "planes", 6)
+            for m in members:
+                nc.scalar.activation(
+                    out=planes[:, m, :], in_=tiles["g", c, n, m][:], func=ACT.Copy, scale=gains[:, 0, c, m : m + 1]
+                )
+
+        def gt_pair_out(c, i):
+            gt_out(c, 1, (2 * i, 2 * i + 1))
+
+        def interleave_gt(c, n):
+            grouped = sbuf(("gt grouped", c, n), [P, CHUNK, MEM], BF16, "planes", 6)
+            src = tiles["gt planes", c, n][:].rearrange("p m f -> p f m")
+            if (c, n) == (0, 0):
+                nc.scalar.copy(out=grouped[:], in_=src)
             else:
-                nc.vector.tensor_copy(out=gg[:], in_=src[:].rearrange("p t n -> p n t"))
+                nc.vector.tensor_copy(out=grouped[:], in_=src)
 
-        def PI(h, c, e="V"):
-            ILV(T["ppl", h, c], ("pg", h, c), e)
-
-        def PQ(h, c):
-            tok = slice(512 * h, 512 * (h + 1))
+        def quantise_gt(c, n):
+            cols = slice(CHUNK * n, CHUNK * (n + 1))
             nc.vector.quantize_mx(
-                out=psq[:, c, tok].bitcast(FP8X4), scales=psqs[:, c, tok], in_=T["pg", h, c][:].rearrange("p n t -> p (n t)")
+                out=gtq[:, c, cols].bitcast(FP8X4),
+                scales=gtq_scales[:, c, cols],
+                in_=tiles["gt grouped", c, n][:].rearrange("p f m -> p (f m)"),
             )
 
-        def G(c, hh, tt, kps=range(KP)):
-            acc = bank(("ga", c, hh, tt), [P, 512], "bk", 8)
-            sl = slice(512 * c + P * tt, 512 * c + P * (tt + 1))
-            cols = slice(512 * hh, 512 * (hh + 1))
-            for kp in kps:
-                nc.tensor.matmul_mx(
-                    out=acc[:],
-                    lhsT=T["wdq", kp][:, sl].bitcast(FP8X4),
-                    lhsT_scale=wdqs[:, kp, sl],
-                    rhs=wq[:, kp, cols].bitcast(FP8X4),
-                    rhs_scale=wqs[:, kp, cols],
-                    start=(kp == 0),
-                    stop=(kp == KP - 1),
+
+        def widen_x(i):
+            x16 = sbuf(("x", i), [P, D], BF16, "x", 2)
+            nc.vector.tensor_tensor(
+                out=x16[:], in0=tiles["x bytes", i][:].bitcast(FP8), in1=x_scale_all[:], op=ALU.mult
+            )
+
+        def transpose_x(i):
+            words = tiles["x", i][:].bitcast(F32)
+            for y in range(2):
+                turned = bank(("x turned", i, y), [P, 2, 2, P])
+                for z in range(2):
+                    w0 = K_PASS // 2 * (2 * y + z)
+                    for u in range(2):
+                        nc.tensor.transpose(turned[:, z, u, :], words[:, w0 + u : w0 + K_PASS // 2 : 2], ident[:])
+
+        def x_out(i):
+            grouped = sbuf(("x grouped", i // 4), [P, PASSES, HALF, 4], BF16, "x_grouped", 2)
+            r0 = P * (i % 4)
+            for y in range(2):
+                nc.scalar.copy(
+                    out=grouped[:].bitcast(F32)[:, 2 * y : 2 * y + 2, r0 : r0 + P, :],
+                    in_=tiles["x turned", i, y][:].rearrange("p z u r -> p z r u"),
                 )
 
-        def GC(c, hh, tt):
-            pl = big(("gpl", c, hh), [P, 4, 512], BF16, "b4", 6)
-            nc.scalar.activation(
-                out=pl[:, tt, :], in_=T["ga", c, hh, tt][:], func=ACT.Copy, scale=vec32[:, 0, c, tt : tt + 1]
-            )
-
-        def GI(c, hh, e="V"):
-            ILV(T["gpl", c, hh], ("gg", c, hh), e)
-
-        def GQ(c, hh):
-            cols = slice(512 * hh, 512 * (hh + 1))
+        def quantise_x(h, y):
+            ks = slice(2 * y, 2 * y + 2)
             nc.vector.quantize_mx(
-                out=gtq[:, c, cols].bitcast(FP8X4), scales=gtqs[:, c, cols], in_=T["gg", c, hh][:].rearrange("p n t -> p (n t)")
+                out=xq[:, h, ks, :].rearrange("p k r -> p (k r)").bitcast(FP8X4),
+                scales=xq_scales[:, h, ks, :].rearrange("p k r -> p (k r)"),
+                in_=tiles["x grouped", h][:, ks].rearrange("p k r j -> p (k r j)"),
             )
 
-        def R(q, c, tp):
-            acc = bank(("ra", q, c, tp), [P, 2, 256], "bk", 8)
-            tok = slice(256 * q, 256 * (q + 1))
-            for ti in range(2):
-                tt = 2 * tp + ti
-                sl = slice(512 * c + P * tt, 512 * c + P * (tt + 1))
-                for kc in range(CH):
+
+        def p_pair(h, c, i):
+            for m in (2 * i, 2 * i + 1):
+                acc = bank(("p", h, c, m), [P, HALF])
+                rows = slice(CHUNK * c + P * m, CHUNK * c + P * (m + 1))
+                for k in range(PASSES):
                     nc.tensor.matmul_mx(
-                        out=acc[:, ti, :],
-                        lhsT=gtq[:, kc, sl].bitcast(FP8X4),
-                        lhsT_scale=gtqs[:, kc, sl],
-                        rhs=psq[:, kc, tok].bitcast(FP8X4),
-                        rhs_scale=psqs[:, kc, tok],
-                        start=(kc == 0),
-                        stop=(kc == CH - 1),
+                        out=acc[:],
+                        lhsT=wq[:, k, rows].bitcast(FP8X4),
+                        lhsT_scale=wq_scales[:, k, rows],
+                        rhs=xq[:, h, k, :].bitcast(FP8X4),
+                        rhs_scale=xq_scales[:, h, k, :],
+                        start=(k == 0),
+                        stop=(k == PASSES - 1),
                     )
 
-        def ST(q, c, tp, e="V"):
-            ht = big(("ht", q, c), [P, 4, 256], F32, "wdq", 4)
-            off = 256 * (q % 2)
-            acc = T["ra", q, c, tp]
-            o = ht[:, 2 * tp : 2 * tp + 2, :]
-            p15 = T["p15", q // 2, c][:, 2 * tp : 2 * tp + 2, off : off + 256]
-            if e == "V":
-                nc.vector.scalar_tensor_tensor(out=o, in0=acc[:], scalar=-0.5, in1=p15, op0=ALU.mult, op1=ALU.add)
-            else:
-                rs = big(("rs", q, c, tp), [P, 2, 256], F32, "xs", 2)
-                nc.scalar.activation(out=rs[:], in_=acc[:], func=ACT.Copy, scale=-0.5)
-                nc.gpsimd.tensor_tensor(out=o, in0=rs[:], in1=p15, op=ALU.add)
+        def p_pair_out(h, c, i):
+            planes = sbuf(("ps planes", h, c), [P, MEM, HALF], BF16, "planes", 6)
+            affine = sbuf(("1.5 p + b", h, c), [P, MEM, HALF], F32, "eight_kib", 4)
+            for m in (2 * i, 2 * i + 1):
+                acc = tiles["p", h, c, m]
+                nc.scalar.activation(
+                    out=planes[:, m, :], in_=acc[:], func=ACT.Copy, scale=gains[:, 1, c, m : m + 1]
+                )
+                nc.scalar.activation(
+                    out=affine[:, m, :], in_=acc[:], func=ACT.Identity, scale=1.5, bias=gains[:, 2, c, m : m + 1]
+                )
 
-        def OT(q, i, c):
-            bk = bank(("ot", q, i, c), [P, 4, P], "bk", 8)
-            for tt in range(4):
-                nc.tensor.transpose(bk[:, tt, :], T["ht", q, c][:, tt, P * i : P * (i + 1)], ident[:])
+        def interleave_ps(h, c):
+            grouped = sbuf(("ps grouped", h, c), [P, HALF, MEM], BF16, "planes", 6)
+            nc.vector.tensor_copy(out=grouped[:], in_=tiles["ps planes", h, c][:].rearrange("p m r -> p r m"))
 
-        def HR(q, i):
-            hr = big(("hr", q, i), [P, 16, 4, 8], F32, "hr", 2)
-            nc.scalar.copy(out=hr[:], in_=T["ot", q, i, 1][:].rearrange("p t (a b) -> p a t b", a=16))
+        def quantise_ps(h, c):
+            tok = slice(HALF * h, HALF * (h + 1))
+            nc.vector.quantize_mx(
+                out=psq[:, c, tok].bitcast(FP8X4),
+                scales=psq_scales[:, c, tok],
+                in_=tiles["ps grouped", h, c][:].rearrange("p r m -> p (r m)"),
+            )
 
-        def MM(q, i):
-            blk = 2 * q + i
-            o = big(("o", q, i), [P, 2, 16, 4, 8], F32, "b4", 6)
-            hl = T["ot", q, i, 0][:].rearrange("p t (a b) -> p a t b", a=16)
-            hr = T["hr", q, i]
-            nc.vector.tensor_tensor(out=o[:, 0], in0=hl, in1=hr[:], op=ALU.max)
-            nc.vector.tensor_tensor(out=o[:, 1], in0=hl, in1=hr[:], op=ALU.min)
-            nc.sync.dma_start(out=out[P * blk : P * (blk + 1), :], in_=o[:].rearrange("p c a t b -> p (c a t b)"))
+
+        def r_chunk(q, c):
+            tok = slice(QUARTER * q, QUARTER * (q + 1))
+            for i in range(2):
+                acc = bank(("r", q, c, i), [P, 2, QUARTER])
+                for z in range(2):
+                    m = 2 * i + z
+                    rows = slice(CHUNK * c + P * m, CHUNK * c + P * (m + 1))
+                    for k in range(CHUNKS):
+                        nc.tensor.matmul_mx(
+                            out=acc[:, z, :],
+                            lhsT=gtq[:, k, rows].bitcast(FP8X4),
+                            lhsT_scale=gtq_scales[:, k, rows],
+                            rhs=psq[:, k, tok].bitcast(FP8X4),
+                            rhs_scale=psq_scales[:, k, tok],
+                            start=(k == 0),
+                            stop=(k == CHUNKS - 1),
+                        )
+
+        def combine(q, c):
+            h_t = sbuf(("h", q, c), [P, MEM, QUARTER], F32, "four_kib", 4)
+            r0 = QUARTER * (q % 2)
+            for i in range(2):
+                members = slice(2 * i, 2 * i + 2)
+                acc = tiles["r", q, c, i]
+                affine = tiles["1.5 p + b", q // 2, c][:, members, r0 : r0 + QUARTER]
+                if (q, c, i) in GPSIMD_SHARE:
+                    half_r = sbuf(("half r", q, c, i), [P, 2, QUARTER], F32, "x", 2)
+                    nc.scalar.activation(out=half_r[:], in_=acc[:], func=ACT.Copy, scale=-0.5)
+                    nc.gpsimd.tensor_tensor(out=h_t[:, members, :], in0=half_r[:], in1=affine, op=ALU.add)
+                else:
+                    nc.vector.scalar_tensor_tensor(
+                        out=h_t[:, members, :], in0=acc[:], scalar=-0.5, in1=affine, op0=ALU.mult, op1=ALU.add
+                    )
+
+
+        def transpose_h(q, i):
+            for c in (1, 0):
+                turned = bank(("h turned", q, i, c), [P, MEM, P])
+                for m in range(MEM):
+                    nc.tensor.transpose(turned[:, m, :], tiles["h", q, c][:, m, P * i : P * (i + 1)], ident[:])
+
+        def by_channel(turned):
+            return turned[:].rearrange("p m (a e) -> p a m e", a=A)
+
+        def copy_right(q, i):
+            right = sbuf(("right", q, i), [P, A, MEM, E], F32, "right", 2)
+            nc.scalar.copy(out=right[:], in_=by_channel(tiles["h turned", q, i, 1]))
+
+        def max_min(q, i):
+            res = sbuf(("result", q, i), [P, 2, A, MEM, E], F32, "planes", 6)
+            tok = slice(QUARTER * q + P * i, QUARTER * q + P * (i + 1))
+            for c, op in enumerate((ALU.max, ALU.min)):
+                nc.vector.tensor_tensor(
+                    out=res[:, c], in0=by_channel(tiles["h turned", q, i, 0]), in1=tiles["right", q, i][:], op=op
+                )
+                nc.sync.dma_start(
+                    out=out[tok, CHUNK * c : CHUNK * (c + 1)], in_=res[:, c].rearrange("p a m e -> p (a m e)")
+                )
 
         ctx.enter_context(tc.manual_schedule())
-        LW(0)
-        WI(0, 0, 0, 1, "S")
-        WI(0, 0, 1, 1, "V")
-        WI(0, 1, 0, 1, "S")
-        WI(0, 0, 2, 1, "V")
-        LW(1)
-        LW(2)
-        WI(0, 0, 3, 1, "V")
-        WI(1, 0, 0, 1, "S")
-        WI(1, 0, 1, 1, "S")
-        WI(0, 1, 1, 1, "V")
-        WI(1, 1, 0, 1, "S")
-        WI(0, 1, 2, 1, "V")
-        WI(1, 1, 1, 1, "S")
-        WI(0, 1, 3, 1, "V")
-        WI(1, 0, 2, 1, "V")
-        WI(1, 1, 2, 1, "S")
-        WQ(0)
-        LW(3)
-        WI(1, 0, 3, 1, "S")
-        WI(2, 1, 0, 1, "S")
-        WI(2, 0, 0, 1, "S")
-        WD(0)
-        WI(1, 1, 3, 1, "V")
-        WDQ(0)
-        LX(1)
-        WI(2, 1, 1, 1, "S")
-        WI(2, 0, 1, 1, "V")
-        WD(1)
-        WI(3, 1, 0, 1, "S")
-        WI(2, 1, 2, 1, "S")
-        VEC()
-        G(0, 0, 2, (0,))
-        LX(3)
-        WQ(1)
-        G(0, 0, 1, (0,))
-        LX(4)
-        WDQ(1)
-        WI(2, 0, 2, 1, "S")
-        WI(2, 1, 3, 1, "S")
-        G(1, 0, 1, (0,))
-        G(0, 0, 3, (0,))
-        WI(2, 0, 3, 1, "S")
-        WD(2)
-        G(1, 0, 2, (0,))
-        WI(3, 1, 1, 1, "S")
-        G(0, 0, 1, (1,))
-        WQ(2)
-        G(1, 0, 0, (0,))
-        WI(3, 1, 2, 1, "S")
-        G(0, 0, 3, (1,))
-        WI(3, 0, 0, 1, "V")
-        WI(3, 0, 1, 1, "S")
-        WI(3, 0, 2, 1, "S")
-        G(0, 0, 2, (1,))
-        WDQ(2)
-        G(1, 0, 1, (1,))
-        WI(3, 1, 3, 1, "S")
-        G(1, 0, 2, (1,))
-        G(1, 0, 3, (0,))
-        LSC()
-        G(0, 0, 0, (0,))
-        G(0, 0, 1, (2,))
-        G(1, 0, 2, (2,))
-        WI(3, 0, 3, 1, "S")
-        G(1, 0, 1, (2,))
-        G(1, 0, 0, (1,))
-        WD(3)
-        G(0, 0, 0, (1,))
-        WQ(3)
-        G(1, 0, 3, (1,))
-        WDQ(3)
-        G(1, 0, 0, (2,))
-        G(0, 0, 0, (2,))
-        G(1, 0, 3, (2,))
-        G(0, 0, 3, (2,))
-        G(1, 0, 1, (3,))
-        G(0, 0, 0, (3,))
-        GC(0, 0, 0)
-        G(1, 0, 3, (3,))
-        LX(0)
-        G(1, 0, 2, (3,))
-        XP(0)
-        G(0, 0, 3, (3,))
-        G(0, 0, 2, (2,))
-        GC(0, 0, 3)
-        GC(1, 0, 2)
-        G(0, 0, 1, (3,))
-        GC(1, 0, 3)
-        LX(2)
-        G(1, 0, 0, (3,))
-        GC(1, 0, 0)
-        G(0, 1, 2)
-        XP(1)
-        LX(7)
-        XT(0, 1)
-        GC(1, 0, 1)
-        XT(0, 0)
-        XC(0, 0)
-        XT(1, 0)
-        G(0, 0, 2, (3,))
-        XP(3)
-        XC(1, 0)
-        G(1, 1, 2)
-        XT(1, 1)
-        XP(2)
-        XT(3, 1)
-        XT(3, 0)
-        LX(5)
-        XC(0, 1)
-        G(0, 1, 3)
-        GC(0, 0, 1)
-        GC(0, 1, 3)
-        XC(3, 0)
-        G(0, 1, 1)
-        XP(5)
-        XT(2, 0)
-        XT(2, 1)
-        GC(0, 1, 2)
-        G(1, 1, 0)
-        LX(6)
-        XP(4)
-        GC(0, 0, 2)
-        G(1, 1, 1)
-        XC(2, 0)
-        XC(1, 1)
-        XC(2, 1)
-        XQ(0, 0)
-        XT(5, 1)
-        XT(5, 0)
-        XT(4, 1)
-        XC(3, 1)
-        GC(1, 1, 0)
-        XQ(0, 1)
-        XC(4, 1)
-        XT(4, 0)
-        PM(0, 3)
-        XC(4, 0)
-        PM(0, 2)
-        XC(5, 1)
-        PM(0, 1)
-        PM(0, 7)
-        XP(7)
-        XP(6)
-        PC(0, 3)
-        GC(1, 1, 1)
-        PM(0, 0)
-        PC(0, 2)
-        XT(6, 0)
-        GC(1, 1, 2)
-        XT(7, 1)
-        PC(0, 1)
-        XT(6, 1)
-        GC(0, 1, 1)
-        XT(7, 0)
-        GI(0, 0, 'V')
-        XC(5, 0)
-        XC(6, 1)
-        PM(0, 4)
-        G(0, 1, 0)
-        PM(0, 6)
-        XC(7, 0)
-        PM(0, 5)
-        GI(1, 0, 'V')
-        XC(7, 1)
-        G(1, 1, 3)
-        XC(6, 0)
-        GQ(0, 0)
-        XQ(1, 1)
-        XQ(1, 0)
-        PC(0, 4)
-        PC(0, 0)
-        PC(0, 7)
-        GC(0, 1, 0)
-        PM(1, 4)
-        PI(0, 0, 'V')
-        PC(0, 6)
-        PC(0, 5)
-        GQ(1, 0)
-        PM(1, 5)
-        PM(1, 1)
-        PQ(0, 0)
-        GI(0, 1, 'V')
-        GC(1, 1, 3)
-        PC(1, 1)
-        PM(1, 3)
-        PI(0, 1, 'V')
-        PC(1, 4)
-        GQ(0, 1)
-        PQ(0, 1)
-        PM(1, 7)
-        PC(1, 5)
-        GI(1, 1, 'V')
-        GQ(1, 1)
-        PM(1, 6)
-        PC(1, 3)
-        PC(1, 7)
-        R(0, 0, 0)
-        R(0, 0, 1)
-        R(0, 1, 0)
-        ST(0, 0, 0, 'V')
-        R(0, 1, 1)
-        ST(0, 1, 0, 'V')
-        ST(0, 0, 1, 'V')
-        PC(1, 6)
-        PM(1, 2)
-        PM(1, 0)
-        ST(0, 1, 1, 'V')
-        PC(1, 2)
-        R(1, 0, 1)
-        R(1, 0, 0)
-        PI(1, 1, 'V')
-        PQ(1, 1)
-        PC(1, 0)
-        PI(1, 0, 'V')
-        OT(0, 1, 1)
-        OT(0, 1, 0)
-        OT(0, 0, 1)
-        PQ(1, 0)
-        OT(0, 0, 0)
-        ST(1, 0, 0, 'G')
-        R(1, 1, 0)
-        R(1, 1, 1)
-        ST(1, 0, 1, 'V')
-        HR(0, 1)
-        MM(0, 1)
-        R(3, 0, 1)
-        ST(1, 1, 1, 'G')
-        ST(1, 1, 0, 'V')
-        R(2, 0, 0)
-        R(2, 1, 0)
-        R(2, 0, 1)
-        HR(0, 0)
-        R(2, 1, 1)
-        OT(1, 0, 1)
-        ST(2, 1, 0, 'G')
-        OT(1, 0, 0)
-        MM(0, 0)
-        ST(3, 0, 1, 'V')
-        OT(1, 1, 1)
-        ST(2, 0, 0, 'G')
-        HR(1, 0)
-        HR(1, 1)
-        OT(1, 1, 0)
-        R(3, 0, 0)
-        ST(2, 1, 1, 'V')
-        MM(1, 0)
-        OT(2, 0, 1)
-        R(3, 1, 0)
-        MM(1, 1)
-        ST(2, 0, 1, 'G')
-        R(3, 1, 1)
-        OT(2, 1, 1)
-        ST(3, 0, 0, 'V')
-        HR(2, 0)
-        ST(3, 1, 0, 'G')
-        ST(3, 1, 1, 'V')
-        OT(2, 0, 0)
-        OT(3, 0, 0)
-        OT(2, 1, 0)
-        MM(2, 0)
-        HR(2, 1)
-        OT(3, 1, 1)
-        OT(3, 1, 0)
-        OT(3, 0, 1)
-        HR(3, 1)
-        MM(2, 1)
-        HR(3, 0)
-        MM(3, 1)
-        MM(3, 0)
+
+        for k in range(PASSES):
+            load_w(k)
+        load_x_scale()
+        for i in (0, 1, 2, 4):
+            load_x(i)
+
+        interleave_w(0)
+        load_gains()
+        interleave_w(1)
+        make_wd(0)
+        quantise_w(0)
+        quantise_wd(0)
+        make_wd(1)
+        interleave_w(2)
+        turn_gains()
+        g_sweep(0)
+        quantise_wd(1)
+        quantise_w(1)
+        quantise_w(2)
+        make_wd(2)
+        interleave_w(3)
+        g_sweep(1)
+        quantise_wd(2)
+        g_sweep(2)
+        make_wd(3)
+        quantise_w(3)
+        quantise_wd(3)
+        widen_x(0)
+        g_sweep(3)
+        widen_x(1)
+
+        gt_out(0, 0, range(MEM))
+        transpose_x(0)
+        x_out(0)
+        load_x(5)
+        widen_x(2)
+        g_pair(0, 0)
+        transpose_x(1)
+        gt_out(1, 0, range(MEM))
+        load_x(3)
+        widen_x(4)
+        g_pair(1, 0)
+        x_out(1)
+        transpose_x(2)
+        interleave_gt(0, 0)
+        x_out(2)
+        load_x(6)
+        widen_x(5)
+        transpose_x(4)
+        gt_pair_out(0, 0)
+        widen_x(3)
+        g_pair(1, 1)
+        transpose_x(5)
+        x_out(4)
+        load_x(7)
+        widen_x(6)
+        transpose_x(3)
+        gt_pair_out(1, 0)
+        x_out(3)
+        gt_pair_out(1, 1)
+        g_pair(0, 1)
+        x_out(5)
+        transpose_x(6)
+        quantise_x(0, 0)
+        quantise_x(0, 1)
+        widen_x(7)
+        x_out(6)
+        interleave_gt(1, 0)
+        gt_pair_out(0, 1)
+
+        p_pair(0, 0, 0)
+        p_pair(0, 0, 1)
+        p_pair_out(0, 0, 0)
+        interleave_gt(0, 1)
+        interleave_gt(1, 1)
+        transpose_x(7)
+        quantise_gt(1, 0)
+        p_pair(0, 1, 0)
+        x_out(7)
+        quantise_x(1, 1)
+        quantise_x(1, 0)
+        p_pair_out(0, 0, 1)
+        p_pair(0, 1, 1)
+        interleave_ps(0, 0)
+        quantise_gt(0, 0)
+        quantise_gt(1, 1)
+        p_pair(1, 0, 0)
+        p_pair_out(0, 1, 0)
+        p_pair(1, 1, 0)
+        quantise_gt(0, 1)
+        p_pair_out(0, 1, 1)
+        interleave_ps(0, 1)
+        p_pair(1, 0, 1)
+        quantise_ps(0, 1)
+        p_pair_out(1, 0, 0)
+        p_pair_out(1, 0, 1)
+        quantise_ps(0, 0)
+
+        r_chunk(1, 0)
+        r_chunk(0, 0)
+        interleave_ps(1, 0)
+        combine(0, 0)
+        r_chunk(0, 1)
+        quantise_ps(1, 0)
+        p_pair(1, 1, 1)
+        combine(0, 1)
+        r_chunk(1, 1)
+        combine(1, 0)
+        transpose_h(0, 0)
+        combine(1, 1)
+        p_pair_out(1, 1, 0)
+        transpose_h(1, 0)
+        p_pair_out(1, 1, 1)
+        transpose_h(0, 1)
+        copy_right(0, 0)
+        interleave_ps(1, 1)
+        quantise_ps(1, 1)
+        copy_right(1, 0)
+        transpose_h(1, 1)
+        max_min(0, 0)
+        copy_right(1, 1)
+
+        r_chunk(2, 0)
+        max_min(1, 0)
+        combine(2, 0)
+        copy_right(0, 1)
+        r_chunk(3, 0)
+        r_chunk(2, 1)
+        max_min(1, 1)
+        r_chunk(3, 1)
+        combine(2, 1)
+        max_min(0, 1)
+        transpose_h(2, 0)
+        combine(3, 0)
+        combine(3, 1)
+        copy_right(2, 0)
+        transpose_h(2, 1)
+        copy_right(2, 1)
+        transpose_h(3, 0)
+        transpose_h(3, 1)
+        max_min(2, 0)
+        copy_right(3, 0)
+        max_min(2, 1)
+        copy_right(3, 1)
+        max_min(3, 0)
+        max_min(3, 1)

from contextlib import ExitStack

import concourse.mybir as mybir
from concourse.masks import make_identity

F32 = mybir.dt.float32
BF16 = mybir.dt.bfloat16
U32 = mybir.dt.uint32
U8 = mybir.dt.uint8
FP8 = mybir.dt.float8_e4m3fn
FP8X4 = mybir.dt.float8_e4m3fn_x4
ALU = mybir.AluOpType
ACT = mybir.ActivationFunctionType

P = 128
N, D, F = 1024, 2048, 1024
K_PASS = 512
PASSES = D // K_PASS
CHUNK = 512
CHUNKS = F // CHUNK
A, MEM, E = 16, 4, 8
HALF = 512
QUARTER = 256
FLOPS = 2 * N * D * F + 2 * D * F * F + 2 * N * F * F

VECTOR_PIECES = (
    ((0, 0), (0, 2), (0, 3), (1, 0), (1, 2), (1, 3)),
    ((0, 1), (0, 3)),
    ((1, 0),),
    ((0, 1),),
)
GPSIMD_SHARE = ((0, 0, 0), (1, 0, 0), (2, 0, 0), (3, 0, 0), (3, 0, 1), (3, 1, 0))


def tile_bjorckmaxmindense_kernel(tc, x_bytes, x_scale, w, d, s, t, b, out):
    nc = tc.nc
    with ExitStack() as ctx:
        keep = ctx.enter_context(tc.tile_pool(name="keep", bufs=1))
        pool = ctx.enter_context(tc.tile_pool(name="pool", bufs=2))
        psum = ctx.enter_context(tc.psum_pool(name="psum", bufs=1))
        tiles = {}

        def sbuf(key, shape, dtype, tag, bufs):
            if key not in tiles:
                tile = pool.tile(shape, dtype, name=tag, tag=tag, bufs=bufs, align_bytes=64)
                tiles[key] = tile
            return tiles[key]

        def bank(key, shape, dtype=F32):
            if key not in tiles:
                tile = psum.tile(shape, dtype, name="bank", tag="bank", bufs=8)
                tiles[key] = tile
            return tiles[key]

        wq = keep.tile([P, PASSES, F], U32, align_bytes=64)
        wq_scales = keep.tile([P, PASSES, F], U8, align_bytes=64)
        wdq_scales = keep.tile([P, PASSES, F], U8, align_bytes=64)
        xq = keep.tile([P, 2, PASSES, HALF], U32, align_bytes=64)
        xq_scales = keep.tile([P, 2, PASSES, HALF], U8, align_bytes=64)
        gtq = keep.tile([P, CHUNKS, F], U32, align_bytes=64)
        gtq_scales = keep.tile([P, CHUNKS, F], U8, align_bytes=64)
        psq = keep.tile([P, CHUNKS, N], U32, align_bytes=64)
        psq_scales = keep.tile([P, CHUNKS, N], U8, align_bytes=64)

        x_scale_all = keep.tile([P, D], F32, align_bytes=64)
        d_sb = keep.tile([P, PASSES, 4], BF16)
        gain_rows = keep.tile([P, A, E], BF16)
        gains = keep.tile([P, 3, CHUNKS, MEM], F32)
        ident16 = keep.tile([P, P], BF16)
        ident = keep.tile([P, P], F32)

        nc.vector.memset(gain_rows[:], 0.0)
        nc.gpsimd.dma_start(out=d_sb[:], in_=d.rearrange("(k p j) -> p k j", p=P, j=4))
        make_identity(nc, ident16[:])
        make_identity(nc, ident[:])


        def load_w(k):
            raw = sbuf(("w raw", k), [P, 4, F], BF16, "eight_kib", 4)
            rows = w[K_PASS * k : K_PASS * (k + 1), :].rearrange("(p j) f -> p j f", j=4)
            if k < 2:
                for c in range(CHUNKS):
                    cols = slice(CHUNK * c, CHUNK * (c + 1))
                    nc.sync.dma_start(out=raw[:, :, cols], in_=rows[:, :, cols])
            else:
                nc.sync.dma_start(out=raw[:], in_=rows)

        def load_x(i):
            codes = sbuf(("x bytes", i), [P, D], U8, "x_bytes", 4)
            nc.sync.dma_start(out=codes[:], in_=x_bytes[P * i : P * (i + 1), :])

        def load_x_scale():
            nc.sync.dma_start(out=x_scale_all[:], in_=x_scale.rearrange("o k -> (o k)").partition_broadcast(P))

        def load_gains():
            for i, v in enumerate((t, s, b)):
                rows = v.rearrange("(c a m e) -> c m a e", c=CHUNKS, a=A, m=MEM)
                for c in range(CHUNKS):
                    r0 = MEM * (CHUNKS * i + c)
                    nc.scalar.dma_start(out=gain_rows[r0 : r0 + MEM], in_=rows[c])

        def turn_gains():
            turned = bank("gains", [P, P], BF16)
            nc.tensor.transpose(turned[:], gain_rows[:].rearrange("p a e -> p (a e)"), ident16[:])
            nc.scalar.copy(out=gains[:].rearrange("p i c m -> p (i c m)"), in_=turned[:, 0 : 3 * CHUNKS * MEM])


        def grouped_w(k):
            return sbuf(("w grouped", k), [P, CHUNKS, MEM, P, 4], BF16, "grouped", 5)

        def interleave_w(k):
            src = tiles["w raw", k][:].rearrange("p j (c a m e) -> p c m a e j", c=CHUNKS, a=A, m=MEM)
            for c in range(CHUNKS):
                for m in range(MEM):
                    dst = grouped_w(k)[:, c, m].rearrange("p (a e) j -> p a e j", a=A)
                    if (c, m) in VECTOR_PIECES[k]:
                        nc.vector.tensor_copy(out=dst, in_=src[:, c, m])
                    else:
                        nc.scalar.copy(out=dst, in_=src[:, c, m])

        def quantise_w(k):
            nc.vector.quantize_mx(
                out=wq[:, k, :].bitcast(FP8X4),
                scales=wq_scales[:, k, :],
                in_=grouped_w(k)[:].rearrange("p c m q j -> p (c m q j)"),
            )

        def make_wd(k):
            wd = sbuf(("wd", k), [P, F, 4], BF16, "grouped", 5)
            nc.vector.tensor_tensor(
                out=wd[:],
                in0=grouped_w(k)[:].rearrange("p c m q j -> p (c m q) j"),
                in1=d_sb[:, k : k + 1, :].to_broadcast([P, F, 4]),
                op=ALU.mult,
            )

        def quantise_wd(k):
            codes = sbuf(("wd codes", k), [P, F], U32, "four_kib", 4)
            nc.vector.quantize_mx(
                out=codes[:].bitcast(FP8X4),
                scales=wdq_scales[:, k, :],
                in_=tiles["wd", k][:].rearrange("p f j -> p (f j)"),
            )


        def g_matmuls(c, n, m, passes):
            acc = bank(("g", c, n, m), [P, CHUNK])
            rows = slice(CHUNK * c + P * m, CHUNK * c + P * (m + 1))
            cols = slice(CHUNK * n, CHUNK * (n + 1))
            for k in passes:
                nc.tensor.matmul_mx(
                    out=acc[:],
                    lhsT=tiles["wd codes", k][:, rows].bitcast(FP8X4),
                    lhsT_scale=wdq_scales[:, k, rows],
                    rhs=wq[:, k, cols].bitcast(FP8X4),
                    rhs_scale=wq_scales[:, k, cols],
                    start=(k == 0),
                    stop=(k == PASSES - 1),
                )

        def g_sweep(k):
            for c in range(CHUNKS):
                for m in range(MEM):
                    g_matmuls(c, 0, m, (k,))

        def g_pair(c, i):
            for m in (2 * i, 2 * i + 1):
                g_matmuls(c, 1, m, range(PASSES))

        def gt_out(c, n, members):
            planes = sbuf(("gt planes", c, n), [P, MEM, CHUNK], BF16, "planes", 6)
            for m in members:
                nc.scalar.activation(
                    out=planes[:, m, :], in_=tiles["g", c, n, m][:], func=ACT.Copy, scale=gains[:, 0, c, m : m + 1]
                )

        def gt_pair_out(c, i):
            gt_out(c, 1, (2 * i, 2 * i + 1))

        def interleave_gt(c, n):
            grouped = sbuf(("gt grouped", c, n), [P, CHUNK, MEM], BF16, "planes", 6)
            src = tiles["gt planes", c, n][:].rearrange("p m f -> p f m")
            if (c, n) == (0, 0):
                nc.scalar.copy(out=grouped[:], in_=src)
            else:
                nc.vector.tensor_copy(out=grouped[:], in_=src)

        def quantise_gt(c, n):
            cols = slice(CHUNK * n, CHUNK * (n + 1))
            nc.vector.quantize_mx(
                out=gtq[:, c, cols].bitcast(FP8X4),
                scales=gtq_scales[:, c, cols],
                in_=tiles["gt grouped", c, n][:].rearrange("p f m -> p (f m)"),
            )


        def widen_x(i):
            x16 = sbuf(("x", i), [P, D], BF16, "x", 2)
            nc.vector.tensor_tensor(
                out=x16[:], in0=tiles["x bytes", i][:].bitcast(FP8), in1=x_scale_all[:], op=ALU.mult
            )

        def transpose_x(i):
            words = tiles["x", i][:].bitcast(F32)
            for y in range(2):
                turned = bank(("x turned", i, y), [P, 2, 2, P])
                for z in range(2):
                    w0 = K_PASS // 2 * (2 * y + z)
                    for u in range(2):
                        nc.tensor.transpose(turned[:, z, u, :], words[:, w0 + u : w0 + K_PASS // 2 : 2], ident[:])

        def x_out(i):
            grouped = sbuf(("x grouped", i // 4), [P, PASSES, HALF, 4], BF16, "x_grouped", 2)
            r0 = P * (i % 4)
            for y in range(2):
                nc.scalar.copy(
                    out=grouped[:].bitcast(F32)[:, 2 * y : 2 * y + 2, r0 : r0 + P, :],
                    in_=tiles["x turned", i, y][:].rearrange("p z u r -> p z r u"),
                )

        def quantise_x(h, y):
            ks = slice(2 * y, 2 * y + 2)
            nc.vector.quantize_mx(
                out=xq[:, h, ks, :].rearrange("p k r -> p (k r)").bitcast(FP8X4),
                scales=xq_scales[:, h, ks, :].rearrange("p k r -> p (k r)"),
                in_=tiles["x grouped", h][:, ks].rearrange("p k r j -> p (k r j)"),
            )


        def p_pair(h, c, i):
            for m in (2 * i, 2 * i + 1):
                acc = bank(("p", h, c, m), [P, HALF])
                rows = slice(CHUNK * c + P * m, CHUNK * c + P * (m + 1))
                for k in range(PASSES):
                    nc.tensor.matmul_mx(
                        out=acc[:],
                        lhsT=wq[:, k, rows].bitcast(FP8X4),
                        lhsT_scale=wq_scales[:, k, rows],
                        rhs=xq[:, h, k, :].bitcast(FP8X4),
                        rhs_scale=xq_scales[:, h, k, :],
                        start=(k == 0),
                        stop=(k == PASSES - 1),
                    )

        def p_pair_out(h, c, i):
            planes = sbuf(("ps planes", h, c), [P, MEM, HALF], BF16, "planes", 6)
            affine = sbuf(("1.5 p + b", h, c), [P, MEM, HALF], F32, "eight_kib", 4)
            for m in (2 * i, 2 * i + 1):
                acc = tiles["p", h, c, m]
                nc.scalar.activation(
                    out=planes[:, m, :], in_=acc[:], func=ACT.Copy, scale=gains[:, 1, c, m : m + 1]
                )
                nc.scalar.activation(
                    out=affine[:, m, :], in_=acc[:], func=ACT.Identity, scale=1.5, bias=gains[:, 2, c, m : m + 1]
                )

        def interleave_ps(h, c):
            grouped = sbuf(("ps grouped", h, c), [P, HALF, MEM], BF16, "planes", 6)
            nc.vector.tensor_copy(out=grouped[:], in_=tiles["ps planes", h, c][:].rearrange("p m r -> p r m"))

        def quantise_ps(h, c):
            tok = slice(HALF * h, HALF * (h + 1))
            nc.vector.quantize_mx(
                out=psq[:, c, tok].bitcast(FP8X4),
                scales=psq_scales[:, c, tok],
                in_=tiles["ps grouped", h, c][:].rearrange("p r m -> p (r m)"),
            )


        def r_chunk(q, c):
            tok = slice(QUARTER * q, QUARTER * (q + 1))
            for i in range(2):
                acc = bank(("r", q, c, i), [P, 2, QUARTER])
                for z in range(2):
                    m = 2 * i + z
                    rows = slice(CHUNK * c + P * m, CHUNK * c + P * (m + 1))
                    for k in range(CHUNKS):
                        nc.tensor.matmul_mx(
                            out=acc[:, z, :],
                            lhsT=gtq[:, k, rows].bitcast(FP8X4),
                            lhsT_scale=gtq_scales[:, k, rows],
                            rhs=psq[:, k, tok].bitcast(FP8X4),
                            rhs_scale=psq_scales[:, k, tok],
                            start=(k == 0),
                            stop=(k == CHUNKS - 1),
                        )

        def combine(q, c):
            h_t = sbuf(("h", q, c), [P, MEM, QUARTER], F32, "four_kib", 4)
            r0 = QUARTER * (q % 2)
            for i in range(2):
                members = slice(2 * i, 2 * i + 2)
                acc = tiles["r", q, c, i]
                affine = tiles["1.5 p + b", q // 2, c][:, members, r0 : r0 + QUARTER]
                if (q, c, i) in GPSIMD_SHARE:
                    half_r = sbuf(("half r", q, c, i), [P, 2, QUARTER], F32, "x", 2)
                    nc.scalar.activation(out=half_r[:], in_=acc[:], func=ACT.Copy, scale=-0.5)
                    nc.gpsimd.tensor_tensor(out=h_t[:, members, :], in0=half_r[:], in1=affine, op=ALU.add)
                else:
                    nc.vector.scalar_tensor_tensor(
                        out=h_t[:, members, :], in0=acc[:], scalar=-0.5, in1=affine, op0=ALU.mult, op1=ALU.add
                    )


        def transpose_h(q, i):
            for c in (1, 0):
                turned = bank(("h turned", q, i, c), [P, MEM, P])
                for m in range(MEM):
                    nc.tensor.transpose(turned[:, m, :], tiles["h", q, c][:, m, P * i : P * (i + 1)], ident[:])

        def by_channel(turned):
            return turned[:].rearrange("p m (a e) -> p a m e", a=A)

        def copy_right(q, i):
            right = sbuf(("right", q, i), [P, A, MEM, E], F32, "right", 2)
            nc.scalar.copy(out=right[:], in_=by_channel(tiles["h turned", q, i, 1]))

        def max_min(q, i):
            res = sbuf(("result", q, i), [P, 2, A, MEM, E], F32, "planes", 6)
            tok = slice(QUARTER * q + P * i, QUARTER * q + P * (i + 1))
            for c, op in enumerate((ALU.max, ALU.min)):
                nc.vector.tensor_tensor(
                    out=res[:, c], in0=by_channel(tiles["h turned", q, i, 0]), in1=tiles["right", q, i][:], op=op
                )
                nc.sync.dma_start(
                    out=out[tok, CHUNK * c : CHUNK * (c + 1)], in_=res[:, c].rearrange("p a m e -> p (a m e)")
                )

        ctx.enter_context(tc.manual_schedule())

        for k in range(PASSES):
            load_w(k)
        load_x_scale()
        for i in (0, 1, 2, 4):
            load_x(i)

        interleave_w(0)
        load_gains()
        interleave_w(1)
        make_wd(0)
        quantise_w(0)
        quantise_wd(0)
        make_wd(1)
        interleave_w(2)
        turn_gains()
        g_sweep(0)
        quantise_wd(1)
        quantise_w(1)
        quantise_w(2)
        make_wd(2)
        interleave_w(3)
        g_sweep(1)
        quantise_wd(2)
        g_sweep(2)
        make_wd(3)
        quantise_w(3)
        quantise_wd(3)
        widen_x(0)
        g_sweep(3)
        widen_x(1)

        gt_out(0, 0, range(MEM))
        transpose_x(0)
        x_out(0)
        load_x(5)
        widen_x(2)
        g_pair(0, 0)
        transpose_x(1)
        gt_out(1, 0, range(MEM))
        load_x(3)
        widen_x(4)
        g_pair(1, 0)
        x_out(1)
        transpose_x(2)
        interleave_gt(0, 0)
        x_out(2)
        load_x(6)
        widen_x(5)
        transpose_x(4)
        gt_pair_out(0, 0)
        widen_x(3)
        g_pair(1, 1)
        transpose_x(5)
        x_out(4)
        load_x(7)
        widen_x(6)
        transpose_x(3)
        gt_pair_out(1, 0)
        x_out(3)
        gt_pair_out(1, 1)
        g_pair(0, 1)
        x_out(5)
        transpose_x(6)
        quantise_x(0, 0)
        quantise_x(0, 1)
        widen_x(7)
        x_out(6)
        interleave_gt(1, 0)
        gt_pair_out(0, 1)

        p_pair(0, 0, 0)
        p_pair(0, 0, 1)
        p_pair_out(0, 0, 0)
        interleave_gt(0, 1)
        interleave_gt(1, 1)
        transpose_x(7)
        quantise_gt(1, 0)
        p_pair(0, 1, 0)
        x_out(7)
        quantise_x(1, 1)
        quantise_x(1, 0)
        p_pair_out(0, 0, 1)
        p_pair(0, 1, 1)
        interleave_ps(0, 0)
        quantise_gt(0, 0)
        quantise_gt(1, 1)
        p_pair(1, 0, 0)
        p_pair_out(0, 1, 0)
        p_pair(1, 1, 0)
        quantise_gt(0, 1)
        p_pair_out(0, 1, 1)
        interleave_ps(0, 1)
        p_pair(1, 0, 1)
        quantise_ps(0, 1)
        p_pair_out(1, 0, 0)
        p_pair_out(1, 0, 1)
        quantise_ps(0, 0)

        r_chunk(1, 0)
        r_chunk(0, 0)
        interleave_ps(1, 0)
        combine(0, 0)
        r_chunk(0, 1)
        quantise_ps(1, 0)
        p_pair(1, 1, 1)
        combine(0, 1)
        r_chunk(1, 1)
        combine(1, 0)
        transpose_h(0, 0)
        combine(1, 1)
        p_pair_out(1, 1, 0)
        transpose_h(1, 0)
        p_pair_out(1, 1, 1)
        transpose_h(0, 1)
        copy_right(0, 0)
        interleave_ps(1, 1)
        quantise_ps(1, 1)
        copy_right(1, 0)
        transpose_h(1, 1)
        max_min(0, 0)
        copy_right(1, 1)

        r_chunk(2, 0)
        max_min(1, 0)
        combine(2, 0)
        copy_right(0, 1)
        r_chunk(3, 0)
        r_chunk(2, 1)
        max_min(1, 1)
        r_chunk(3, 1)
        combine(2, 1)
        max_min(0, 1)
        transpose_h(2, 0)
        combine(3, 0)
        combine(3, 1)
        copy_right(2, 0)
        transpose_h(2, 1)
        copy_right(2, 1)
        transpose_h(3, 0)
        transpose_h(3, 1)
        max_min(2, 0)
        copy_right(3, 0)
        max_min(2, 1)
        copy_right(3, 1)
        max_min(3, 0)
        max_min(3, 1)
